import numpy as np
import ml_dtypes


def mxq(x, axis, fmt="e4m3"):
    dtype, down = {"e4m3": (ml_dtypes.float8_e4m3fn, 7), "e5m2": (ml_dtypes.float8_e5m2, 14)}[fmt]
    v = np.moveaxis(np.asarray(x, np.float32).astype(ml_dtypes.bfloat16).astype(np.float64), axis, -1)
    blocks = v.reshape(v.shape[:-1] + (-1, 32))
    amax = np.abs(blocks).max(-1, keepdims=True)
    byte = np.maximum(np.where(amax > 0, np.frexp(amax)[1] - 1 + 127, 0) - down, 1)
    scale = np.exp2(byte - 127.0)
    codes = (blocks / scale).astype(np.float32).astype(dtype).astype(np.float64)
    return np.moveaxis((codes * scale).reshape(v.shape), -1, axis)


WIDE = False


def mx_kscale(k):
    if not WIDE:
        return np.ones(k)
    levels = np.array([10, -10, 5, -5, 0])
    if k % 512:
        return np.exp2(np.random.permutation(np.resize(levels, k // 32))).repeat(32)
    a = np.empty((k // 512, 16))
    for p in range(k // 512):
        a[p, :8] = np.random.permutation(np.resize(levels, 8))
        for g in range(8):
            far = levels[np.abs(levels - a[p, g]) >= 10]
            a[p, g + 8] = far[np.random.randint(len(far))]
    return np.exp2(a.ravel()).repeat(32)


def f64(x):
    return np.asarray(x).astype(np.float64)


def striped(idx):
    return np.tile(idx.reshape(-1, 16).T, (8, 1)).astype(np.uint16)


def unstriped(offs):
    return offs[:16].T.reshape(-1).astype(np.int64)


def pack_weight(w):
    k, n = w.shape
    w = f64(np.asarray(w, np.float32).astype(ml_dtypes.bfloat16)).reshape(k // 32, 32, n)
    amax = np.abs(w).max(1)
    byte = np.clip(np.where(amax > 0, np.frexp(amax)[1] - 1 + 127 - 7, 1), 1, 254)
    scaled = (w * np.exp2(127.0 - byte)[:, None, :]).reshape(k, n).astype(np.float32)
    words = np.ascontiguousarray(scaled.reshape(k // 512, 128, 4, n).transpose(0, 1, 3, 2)).astype(ml_dtypes.float8_e4m3fn).view(np.uint8)
    return words, np.ascontiguousarray(byte.astype(np.uint8).reshape(k // 512, 16, n))


def unpack_weight(words, scales):
    g, p, n, _ = words.shape
    vals = np.ascontiguousarray(words).view(ml_dtypes.float8_e4m3fn).astype(np.float64) * np.repeat(np.exp2(scales.astype(np.float64) - 127.0), 8, axis=1)[..., None]
    return vals.transpose(0, 1, 3, 2).reshape(g * 512, n)


K, T, S, D, N, H, V, U = 512, 2048, 1024, 4, 256, 512, 256, 512


def setup_inputs():
    n = np.random.standard_normal
    s = mx_kscale(K)[:, None]
    u = mx_kscale(H)
    packed_xT = pack_weight(n((K, T)) * s)
    return {
        "x_words": packed_xT[0],
        "x_scales": packed_xT[1],
        "w1": (n((K, H)) / np.sqrt(K) / s).astype(np.float32),
        "lw": (np.random.uniform(0.5, 1.5, (H, U))).astype(np.float32),
        "unit": (np.random.uniform(0.6, 1.4, (H, 1)) * u[:, None]).astype(np.float32),
        "w2": (n((H, N)) / np.sqrt(H) / u[:, None]).astype(np.float32),
        "offs": striped(np.random.permutation(T)[:S]),
        "shf": striped(np.random.permutation(S)),
        "lag": striped(np.random.permutation(np.concatenate([np.arange(V), np.random.randint(0, V, U - V)]))),
    }


def reference(x_words, x_scales, w1, lw, unit, w2, offs, shf, lag):
    xq = unpack_weight(x_words, x_scales)[:, unstriped(offs)]
    y = mxq(f64(w1), 0, "e4m3").T @ xq
    ys = y[:, unstriped(shf)]
    dif = y - ys
    rootd = np.sqrt(np.abs(dif) + 0.05)
    rmean = rootd.reshape(len(rootd), -1, D).mean(axis=2)
    cress = (((rmean) ** 2) ** 2) / (0.5 * ((rmean) ** 2) + 0.6)
    cl = cress[:, unstriped(lag)]
    cw = cl * f64(lw)
    d2 = (dif) ** 2
    mat = d2.reshape(len(d2), -1, D).mean(axis=2)
    ml = mat[:, unstriped(lag)]
    hid = f64(unit) * (cw - (0.4 * ml))
    return mxq(f64(w2), 0, "e4m3").T @ mxq(hid, 0, "e4m3")

@@ -1,0 +1,288 @@
+from contextlib import ExitStack
+
+import concourse.mybir as mybir
+from concourse.masks import make_identity
+
+K, T, S, D, N, H, V, U = 512, 2048, 1024, 4, 256, 512, 256, 512
+FLOPS = 2 * K * H * S + 2 * H * N * U
+
+F32 = mybir.dt.float32
+BF16 = mybir.dt.bfloat16
+I32 = mybir.dt.int32
+U32 = mybir.dt.uint32
+U16 = mybir.dt.uint16
+U8 = mybir.dt.uint8
+FP8X4 = mybir.dt.float8_e4m3fn_x4
+ACT = mybir.ActivationFunctionType
+ALU = mybir.AluOpType
+AX = mybir.AxisListType
+
+P = 128
+PACK = 4
+BANK = 512
+LIST = 16
+ORDER = "p0 p1 p2 p3 f0 f1 f2 f3 r0 r1 r2 i0 r3 i3 c0 c1 c2 c3 m0 m1 m2 m3 h0 h1 h2 h3 w".split()
+ML, CL, SQ, STEP, AC, IL, NN, HIL, RES = "VVVV", "HHHH", "HHHH", "2222", "SVSSSSSS", "VSVS", "SSSS", "VV", "SS"
+SUB = "PPPP"
+TAIL = 2
+
+
+def tile_picked_yvario_gap_p_kernel(
+    tc, x_words, x_scales, w1, lw, unit, w2, offs, shf, lag, out
+):
+    nc = tc.nc
+    with ExitStack() as ctx:
+        keep = ctx.enter_context(tc.tile_pool(name="keep", bufs=1))
+        work = ctx.enter_context(tc.tile_pool(name="work", bufs=4))
+        psum = ctx.enter_context(tc.psum_pool(name="psum", bufs=1))
+
+        def copy_on(engine, dst, src):
+            if engine == "V":
+                nc.vector.tensor_copy(dst, src)
+            elif engine == "G":
+                nc.gpsimd.tensor_copy(dst, src)
+            else:
+                nc.scalar.copy(dst, src)
+
+        def bank(n):
+            return psum.tile([P, BANK], F32, name="bank%d" % n)
+
+        offs_sb = keep.tile([P, S // LIST], U16, name="offs_sb")
+        shf_sb = keep.tile([P, S // LIST], U16, name="shf_sb")
+        lag_sb = keep.tile([P, U // LIST], U16, name="lag_sb")
+        xs_sb = keep.tile([P, T], U8, name="xs_sb", align_bytes=64)
+        xw_sb = keep.tile([P, T], I32, name="xw_sb", align_bytes=64)
+        w1_sb = keep.tile([P, PACK, H], F32, name="w1_sb")
+        ys = [keep.tile([P, 2 * S], F32, name="y%d" % t) for t in range(PACK)]
+        w2_sb = ys[3][:, S:].rearrange("p (j c) -> p j c", j=PACK)
+        lw_sb = [ys[1 + t // 2][:, S + (t % 2) * U : S + (t % 2 + 1) * U] for t in range(PACK)]
+        unit_sb = keep.tile([P, PACK], F32, name="unit_sb")
+        ident = keep.tile([P, P], F32, name="ident")
+
+        nc.vector.memset(xs_sb[:].bitcast(I32), 0)
+        nc.sync.dma_start(offs_sb[:], offs)
+        nc.sync.dma_start(shf_sb[:], shf)
+        for q in range(4):
+            nc.sync.dma_start(
+                xs_sb[32 * q : 32 * q + 4, :].bitcast(I32),
+                x_scales[0, 4 * q : 4 * q + 4, :].bitcast(I32),
+            )
+        nc.sync.dma_start(xw_sb[:], x_words[0].rearrange("p c r -> p (c r)").bitcast(I32))
+        nc.sync.dma_start(w1_sb[:], w1.rearrange("(p j) c -> p j c", j=PACK))
+        lw_rows = lw.rearrange("(p t) r -> p (t r)", t=PACK)
+        for u in range(2):
+            nc.sync.dma_start(ys[1 + u][:, S:], lw_rows[:, u * S : (u + 1) * S])
+        nc.sync.dma_start(w2_sb, w2.rearrange("(p j) c -> p j c", j=PACK))
+        nc.sync.dma_start(lag_sb[:], lag)
+        nc.sync.dma_start(unit_sb[:], unit.rearrange("(p t) o -> p (t o)", t=PACK))
+        nc.gpsimd.memset(ys[0][:, S:], 0.0)
+        make_identity(nc, ident[:])
+
+        halves = range(S // BANK)
+        x_codes = [keep.tile([P, BANK], U32, name="x_codes%d" % h, align_bytes=64) for h in halves]
+        x_bytes = [keep.tile([P, BANK], U8, name="x_bytes%d" % h, align_bytes=64) for h in halves]
+        per_bank = BANK // LIST
+        for h in halves:
+            nc.vector.tensor_copy(x_bytes[h][:], xs_sb[:].indirect(offs_sb[:, h * per_bank : (h + 1) * per_bank]))
+        for h in halves:
+            nc.vector.tensor_copy(
+                x_codes[h][:], xw_sb[:].bitcast(U32).indirect(offs_sb[:, h * per_bank : (h + 1) * per_bank])
+            )
+
+        w1_dealt = w1_sb[:].rearrange("p j (m t) -> p t m j", t=PACK)
+        w1_codes, w1_bytes = [], []
+        for t in range(PACK):
+            grouped = keep.tile([P, P, PACK], BF16, name="w1_grouped%d" % t, align_bytes=64)
+            copy_on(IL[t], grouped[:], w1_dealt[:, t])
+            codes = keep.tile([P, P], U32, name="w1_codes%d" % t, align_bytes=64)
+            scales = keep.tile([P, P], U8, name="w1_bytes%d" % t, align_bytes=64)
+            nc.vector.quantize_mx(
+                out=codes[:].bitcast(FP8X4), scales=scales[:], in_=grouped[:].rearrange("p m j -> p (m j)")
+            )
+            w1_codes.append(codes)
+            w1_bytes.append(scales)
+
+        def product(t):
+            y = ys[t]
+            for h in halves:
+                acc = bank(2 * t + h)
+                nc.tensor.matmul_mx(
+                    out=acc[:],
+                    lhsT=w1_codes[t][:].bitcast(FP8X4),
+                    lhsT_scale=w1_bytes[t][:],
+                    rhs=x_codes[h][:].bitcast(FP8X4),
+                    rhs_scale=x_bytes[h][:],
+                    start=True,
+                    stop=True,
+                )
+                copy_on(AC[2 * t + h], y[:, h * BANK : (h + 1) * BANK], acc[:])
+
+        w2_grouped = keep.tile([P, N, PACK], BF16, name="w2_grouped", align_bytes=64)
+        w2_codes = keep.tile([P, N], U32, name="w2_codes", align_bytes=64)
+        w2_bytes = keep.tile([P, N], U8, name="w2_bytes", align_bytes=64)
+        mat_factor = keep.tile([P, PACK], F32, name="mat_factor")
+        lag_cut = U // 2
+        lag_cols = lag_cut // LIST
+        all_sums, qs, cresses, banks = {}, {}, {}, {}
+        mags = [keep.tile([P, S], F32, name="mag%d" % t) for t in range(PACK)]
+        inv = keep.tile([P, PACK * V], F32, name="inv")
+        hid = keep.tile([P, PACK, U], BF16, name="hid")
+
+        def front(t):
+            y = ys[t]
+            step = int(STEP[t])
+            neg = work.tile([P, S], F32, name="neg", bufs=4)
+            mag = mags[t]
+            diff = work.tile([P, S], F32, name="diff") if SUB[t] == "G" else None
+            root = work.tile([P, S], F32, name="root")
+            sq = work.tile([P, S], F32, name="sq")
+            for h in halves:
+                cols = slice(h * BANK, (h + 1) * BANK)
+                nc.vector.tensor_scalar(
+                    neg[:, cols],
+                    y[:].indirect(shf_sb[:, h * per_bank : (h + 1) * per_bank]),
+                    -1.0,
+                    0.0,
+                    ALU.mult,
+                    ALU.add,
+                )
+                if SUB[t] == "G":
+                    nc.gpsimd.tensor_tensor(diff[:, cols], y[:, cols], neg[:, cols], ALU.add)
+                dif = bank((2 * t + h) % 6)
+                for b in range(D // step):
+                    for e in range(step):
+                        first = h * BANK + step * P * b
+                        picked = slice(first + e, first + step * P, step)
+                        block = dif[:, (step * b + e) * P : (step * b + e + 1) * P]
+                        if SUB[t] == "G":
+                            nc.tensor.matmul(block, diff[:, picked], ident[:], start=True, stop=True, is_transpose=True)
+                            continue
+                        nc.tensor.matmul(block, y[:, picked], ident[:], start=True, stop=False, is_transpose=True)
+                        nc.tensor.matmul(block, neg[:, picked], ident[:], start=False, stop=True, is_transpose=True)
+                nc.scalar.activation(mag[:, cols], dif[:], ACT.Abs)
+                nc.scalar.activation(root[:, cols], mag[:, cols], ACT.Sqrt, bias=0.05)
+                if SQ[t] == "S" or (SQ[t] == "H" and h == 0):
+                    nc.scalar.activation(sq[:, cols], dif[:], ACT.Square)
+                elif SQ[t] == "G":
+                    nc.gpsimd.tensor_tensor(sq[:, cols], mag[:, cols], mag[:, cols], ALU.mult)
+                else:
+                    nc.vector.tensor_tensor(sq[:, cols], mag[:, cols], mag[:, cols], ALU.mult)
+
+            sums = keep.tile([P, 2 * V], F32, name="sums%d" % t)
+            for src, tag, place in ((root, "root_pairs", 1), (sq, "sq_pairs", 0)):
+                pairs = bank(6 + place)
+                for g in range(S // P // step):
+                    for e in range(step):
+                        nc.tensor.matmul(
+                            pairs[:, g * P : (g + 1) * P],
+                            src[:, (step * g + e) * P : (step * g + e + 1) * P],
+                            ident[:],
+                            start=(e == 0),
+                            stop=(e == step - 1),
+                            is_transpose=True,
+                        )
+                if step == 2:
+                    nc.vector.tensor_reduce(
+                        sums[:, place * V : (place + 1) * V], pairs[:].rearrange("p (v d) -> p v d", d=2), AX.X, ALU.add
+                    )
+                else:
+                    copy_on("V", sums[:, place * V : (place + 1) * V], pairs[:, :V])
+            all_sums[t] = sums
+
+        dens = keep.tile([P, PACK * V], F32, name="dens")
+        early = (PACK - 1) * V
+
+        def robust(t):
+            q = mags[min(t + 1, PACK - 1)][:, BANK + (t % 2) * V : BANK + (t % 2 + 1) * V]
+            nc.scalar.activation(q, all_sums[t][:, V:], ACT.Square, scale=1.0 / D)
+            cress = keep.tile([P, 2 * V], F32, name="cress%d" % t)
+            nc.scalar.activation(dens[:, t * V : (t + 1) * V], q, ACT.Square, scale=0.5, bias=0.6)
+            if NN[t] == "S":
+                nc.scalar.activation(cress[:, V:], q, ACT.Square)
+            elif NN[t] == "G":
+                nc.gpsimd.tensor_tensor(cress[:, V:], q, q, ALU.mult)
+            else:
+                nc.vector.tensor_tensor(cress[:, V:], q, q, ALU.mult)
+            cresses[t] = cress
+
+        def inverse(t):
+            cols = slice(0, early) if t == 0 else slice(early, PACK * V)
+            nc.scalar.activation(inv[:, cols], dens[:, cols], ACT.Abs_reciprocal_sqrt)
+
+        def cressie(t):
+            cress = cresses[t]
+            nc.vector.scalar_tensor_tensor(
+                cress[:, :V], cress[:, V:], unit_sb[:, t : t + 1], inv[:, t * V : (t + 1) * V], ALU.mult, ALU.mult
+            )
+
+        mls = {}
+
+        def matheron(t):
+            ml = keep.tile([P, U], F32, name="ml%d" % t)
+            for c in range(2):
+                cols = slice(c * lag_cut, (c + 1) * lag_cut)
+                lags = lag_sb[:, c * lag_cols : (c + 1) * lag_cols]
+                if ML[t] == "V" or (ML[t] == "H" and c == 0):
+                    nc.vector.tensor_copy(ml[:, cols], all_sums[t][:].indirect(lags))
+                else:
+                    nc.scalar.activation(ml[:, cols], all_sums[t][:].indirect(lags), ACT.Copy)
+            mls[t] = ml
+
+        def hidden(t):
+            if t not in mls:
+                matheron(t)
+            cress = cresses[t]
+            ml = mls[t]
+            cw = keep.tile([P, U], F32, name="cw%d" % t)
+            cl = keep.tile([P, U], F32, name="cl%d" % t)
+            for c in range(2):
+                cols = slice(c * lag_cut, (c + 1) * lag_cut)
+                lags = lag_sb[:, c * lag_cols : (c + 1) * lag_cols]
+                if CL[t] == "F" or (CL[t] == "H" and c == 1):
+                    nc.vector.tensor_tensor(cw[:, cols], cress[:].indirect(lags), lw_sb[t][:, cols], ALU.mult)
+                else:
+                    nc.scalar.activation(cl[:, cols], cress[:].indirect(lags), ACT.Copy)
+                    nc.vector.tensor_tensor(cw[:, cols], cl[:, cols], lw_sb[t][:, cols], ALU.mult)
+                nc.vector.scalar_tensor_tensor(
+                    hid[:, t, cols], ml[:, cols], mat_factor[:, t : t + 1], cw[:, cols], ALU.mult, ALU.add
+                )
+
+        def second_weights(t):
+            copy_on("S", w2_grouped[:], w2_sb.rearrange("p j n -> p n j"))
+            nc.vector.quantize_mx(
+                out=w2_codes[:].bitcast(FP8X4), scales=w2_bytes[:], in_=w2_grouped[:].rearrange("p n j -> p (n j)")
+            )
+
+        nc.vector.tensor_scalar(mat_factor[:], unit_sb[:], -0.4 / D, None, ALU.mult)
+        stages = {"p": product, "f": front, "r": robust, "m": matheron, "h": hidden, "w": second_weights, "i": inverse, "c": cressie}
+        if "p0" not in ORDER:
+            for t in range(PACK):
+                product(t)
+        for item in ORDER:
+            stages[item[0]](int(item[1:] or 0))
+
+        out_blocks = out.rearrange("(b p) r -> p b r", p=P)
+        width = U // TAIL
+        for c in range(TAIL):
+            cols = slice(c * width, (c + 1) * width)
+            grouped = keep.tile([P, width, PACK], BF16, name="hid_grouped%d" % c, align_bytes=64)
+            copy_on(HIL[c], grouped[:], hid[:, :, cols].rearrange("p t r -> p r t"))
+            codes = keep.tile([P, width], U32, name="hid_codes%d" % c, align_bytes=64)
+            scales = keep.tile([P, width], U8, name="hid_bytes%d" % c, align_bytes=64)
+            nc.vector.quantize_mx(
+                out=codes[:].bitcast(FP8X4), scales=scales[:], in_=grouped[:].rearrange("p r t -> p (r t)")
+            )
+            acc = bank(2 + c)
+            for b in range(N // P):
+                nc.tensor.matmul_mx(
+                    out=acc[:, b * width : (b + 1) * width],
+                    lhsT=w2_codes[:, b * P : (b + 1) * P].bitcast(FP8X4),
+                    lhsT_scale=w2_bytes[:, b * P : (b + 1) * P],
+                    rhs=codes[:].bitcast(FP8X4),
+                    rhs_scale=scales[:],
+                    start=True,
+                    stop=True,
+                )
+            result = keep.tile([P, N // P, width], F32, name="result%d" % c)
+            copy_on(RES[c], result[:].rearrange("p b r -> p (b r)"), acc[:, : N // P * width])
+            nc.sync.dma_start(out_blocks[:, :, cols], result[:])

@@ -21,9 +21,11 @@ P = 128
 PACK = 4
 BANK = 512
 LIST = 16
-ORDER = "p0 p1 p2 p3 f0 f1 f2 f3 r0 r1 r2 i0 r3 i3 c0 c1 c2 c3 m0 m1 m2 m3 h0 h1 h2 h3 w".split()
-ML, CL, SQ, STEP, AC, IL, NN, HIL, RES = "VVVV", "HHHH", "HHHH", "2222", "SVSSSSSS", "VSVS", "SSSS", "VV", "SS"
+ORDER = "p0 p1 p2 p3 w f0 f1 f2 R0 f3 R1 s0 D0 s1 D1 R2 R3 r0 r1 i01 c0 c1 r2 i2 c2 r3 i3 c3 s2 D2 s3 D3 m0 m1 m2 m3 H0 H1".split()
+ML, CL, SQ, STEP, AC, IL, NN, HIL, RES = "", "", "", "2222", "SVSSSSSS", "VSVS", "SSSS", "SV", "SS"
 SUB = "PPPP"
+CUTS, MLS, CLS = [0,256,512], ["VVVS","VVVS"], ["SSSS","SSFF"]
+SQS = ["VV","VV","VV","VS"]
 TAIL = 2
 
 
@@ -92,7 +94,7 @@ def tile_picked_yvario_gap_p_kernel(
         w1_dealt = w1_sb[:].rearrange("p j (m t) -> p t m j", t=PACK)
         w1_codes, w1_bytes = [], []
         for t in range(PACK):
-            grouped = keep.tile([P, P, PACK], BF16, name="w1_grouped%d" % t, align_bytes=64)
+            grouped = keep.tile([P, P, PACK], BF16, name="w1_grouped%d" % (0 if t == 2 else t), align_bytes=64)
             copy_on(IL[t], grouped[:], w1_dealt[:, t])
             codes = keep.tile([P, P], U32, name="w1_codes%d" % t, align_bytes=64)
             scales = keep.tile([P, P], U8, name="w1_bytes%d" % t, align_bytes=64)
@@ -125,8 +127,6 @@ def tile_picked_yvario_gap_p_kernel(
         lag_cols = lag_cut // LIST
         all_sums, qs, cresses, banks = {}, {}, {}, {}
         mags = [keep.tile([P, S], F32, name="mag%d" % t) for t in range(PACK)]
-        inv = keep.tile([P, PACK * V], F32, name="inv")
-        hid = keep.tile([P, PACK, U], BF16, name="hid")
 
         def front(t):
             y = ys[t]
@@ -161,39 +161,44 @@ def tile_picked_yvario_gap_p_kernel(
                         nc.tensor.matmul(block, neg[:, picked], ident[:], start=False, stop=True, is_transpose=True)
                 nc.scalar.activation(mag[:, cols], dif[:], ACT.Abs)
                 nc.scalar.activation(root[:, cols], mag[:, cols], ACT.Sqrt, bias=0.05)
-                if SQ[t] == "S" or (SQ[t] == "H" and h == 0):
+                if SQS[t][h] == "S":
                     nc.scalar.activation(sq[:, cols], dif[:], ACT.Square)
-                elif SQ[t] == "G":
-                    nc.gpsimd.tensor_tensor(sq[:, cols], mag[:, cols], mag[:, cols], ALU.mult)
-                else:
-                    nc.vector.tensor_tensor(sq[:, cols], mag[:, cols], mag[:, cols], ALU.mult)
 
-            sums = keep.tile([P, 2 * V], F32, name="sums%d" % t)
-            for src, tag, place in ((root, "root_pairs", 1), (sq, "sq_pairs", 0)):
-                pairs = bank(6 + place)
-                for g in range(S // P // step):
-                    for e in range(step):
-                        nc.tensor.matmul(
-                            pairs[:, g * P : (g + 1) * P],
-                            src[:, (step * g + e) * P : (step * g + e + 1) * P],
-                            ident[:],
-                            start=(e == 0),
-                            stop=(e == step - 1),
-                            is_transpose=True,
-                        )
-                if step == 2:
-                    nc.vector.tensor_reduce(
-                        sums[:, place * V : (place + 1) * V], pairs[:].rearrange("p (v d) -> p v d", d=2), AX.X, ALU.add
+            banks[t] = (root, sq)
+
+        def square(t):
+            for h in halves:
+                cols = slice(h * BANK, (h + 1) * BANK)
+                if SQS[t][h] != "S":
+                    (nc.gpsimd if SQS[t][h] == "G" else nc.vector).tensor_tensor(banks[t][1][:, cols], mags[t][:, cols], mags[t][:, cols], ALU.mult)
+
+        for t in range(PACK):
+            all_sums[t] = keep.tile([P, 2 * V], F32, name="sums%d" % t)
+
+        def back(t, place):
+            src = banks[t][1 - place]
+            pairs = bank(([2,3,4,5], [6,7,6,7])[place][t])
+            for g in range(S // P // 2):
+                for e in range(2):
+                    nc.tensor.matmul(
+                        pairs[:, g * P : (g + 1) * P],
+                        src[:, (2 * g + e) * P : (2 * g + e + 1) * P],
+                        ident[:],
+                        start=(e == 0),
+                        stop=(e == 1),
+                        is_transpose=True,
                     )
-                else:
-                    copy_on("V", sums[:, place * V : (place + 1) * V], pairs[:, :V])
-            all_sums[t] = sums
+            nc.vector.tensor_reduce(
+                all_sums[t][:, place * V : (place + 1) * V], pairs[:].rearrange("p (v d) -> p v d", d=2), AX.X, ALU.add
+            )
 
         dens = keep.tile([P, PACK * V], F32, name="dens")
+        inv01 = mags[PACK - 1][:, BANK:]
         early = (PACK - 1) * V
 
         def robust(t):
-            q = mags[min(t + 1, PACK - 1)][:, BANK + (t % 2) * V : BANK + (t % 2 + 1) * V]
+            hold = [9,9,9,9][t]
+            q = mags[hold][:, BANK : BANK + V] if hold < PACK else keep.tile([P, V], F32, name="q%d" % t)[:]
             nc.scalar.activation(q, all_sums[t][:, V:], ACT.Square, scale=1.0 / D)
             cress = keep.tile([P, 2 * V], F32, name="cress%d" % t)
             nc.scalar.activation(dens[:, t * V : (t + 1) * V], q, ACT.Square, scale=0.5, bias=0.6)
@@ -205,74 +210,54 @@ def tile_picked_yvario_gap_p_kernel(
                 nc.vector.tensor_tensor(cress[:, V:], q, q, ALU.mult)
             cresses[t] = cress
 
-        def inverse(t):
-            cols = slice(0, early) if t == 0 else slice(early, PACK * V)
-            nc.scalar.activation(inv[:, cols], dens[:, cols], ACT.Abs_reciprocal_sqrt)
+        def inverse(tiles):
+            cols = slice(tiles[0] * V, (tiles[-1] + 1) * V)
+            place = inv01 if tiles[0] == 0 else dens[:, (tiles[0] - 2) * V : (tiles[-1] - 1) * V]
+            nc.scalar.activation(place, dens[:, cols], ACT.Abs_reciprocal_sqrt)
 
         def cressie(t):
             cress = cresses[t]
+            inv = inv01[:, t * V : (t + 1) * V] if t < 2 else dens[:, (t - 2) * V : (t - 1) * V]
             nc.vector.scalar_tensor_tensor(
-                cress[:, :V], cress[:, V:], unit_sb[:, t : t + 1], inv[:, t * V : (t + 1) * V], ALU.mult, ALU.mult
+                cress[:, :V], cress[:, V:], unit_sb[:, t : t + 1], inv, ALU.mult, ALU.mult
             )
 
-        mls = {}
+        mls = [keep.tile([P, U], F32, name="ml%d" % t) for t in range(PACK)]
+        cws = [keep.tile([P, U], F32, name="cw%d" % t) for t in range(PACK)]
+        cls = [keep.tile([P, U], F32, name="cl%d" % t) for t in range(PACK)]
+        out_blocks = out.rearrange("(b p) r -> p b r", p=P)
 
         def matheron(t):
-            ml = keep.tile([P, U], F32, name="ml%d" % t)
             for c in range(2):
                 cols = slice(c * lag_cut, (c + 1) * lag_cut)
                 lags = lag_sb[:, c * lag_cols : (c + 1) * lag_cols]
-                if ML[t] == "V" or (ML[t] == "H" and c == 0):
-                    nc.vector.tensor_copy(ml[:, cols], all_sums[t][:].indirect(lags))
+                if MLS[c][t] == "V":
+                    nc.vector.tensor_copy(mls[t][:, cols], all_sums[t][:].indirect(lags))
                 else:
-                    nc.scalar.activation(ml[:, cols], all_sums[t][:].indirect(lags), ACT.Copy)
-            mls[t] = ml
+                    nc.scalar.activation(mls[t][:, cols], all_sums[t][:].indirect(lags), ACT.Copy)
 
-        def hidden(t):
-            if t not in mls:
-                matheron(t)
-            cress = cresses[t]
-            ml = mls[t]
-            cw = keep.tile([P, U], F32, name="cw%d" % t)
-            cl = keep.tile([P, U], F32, name="cl%d" % t)
-            for c in range(2):
-                cols = slice(c * lag_cut, (c + 1) * lag_cut)
-                lags = lag_sb[:, c * lag_cols : (c + 1) * lag_cols]
-                if CL[t] == "F" or (CL[t] == "H" and c == 1):
-                    nc.vector.tensor_tensor(cw[:, cols], cress[:].indirect(lags), lw_sb[t][:, cols], ALU.mult)
-                else:
-                    nc.scalar.activation(cl[:, cols], cress[:].indirect(lags), ACT.Copy)
-                    nc.vector.tensor_tensor(cw[:, cols], cl[:, cols], lw_sb[t][:, cols], ALU.mult)
-                nc.vector.scalar_tensor_tensor(
-                    hid[:, t, cols], ml[:, cols], mat_factor[:, t : t + 1], cw[:, cols], ALU.mult, ALU.add
-                )
-
-        def second_weights(t):
-            copy_on("S", w2_grouped[:], w2_sb.rearrange("p j n -> p n j"))
-            nc.vector.quantize_mx(
-                out=w2_codes[:].bitcast(FP8X4), scales=w2_bytes[:], in_=w2_grouped[:].rearrange("p n j -> p (n j)")
-            )
-
-        nc.vector.tensor_scalar(mat_factor[:], unit_sb[:], -0.4 / D, None, ALU.mult)
-        stages = {"p": product, "f": front, "r": robust, "m": matheron, "h": hidden, "w": second_weights, "i": inverse, "c": cressie}
-        if "p0" not in ORDER:
+        def hidden(c):
+            cols = slice(CUTS[c], CUTS[c + 1])
+            width = CUTS[c + 1] - CUTS[c]
+            lags = lag_sb[:, CUTS[c] // LIST : CUTS[c + 1] // LIST]
+            hid = keep.tile([P, PACK, width], BF16, name="hid%d" % c)
             for t in range(PACK):
-                product(t)
-        for item in ORDER:
-            stages[item[0]](int(item[1:] or 0))
-
-        out_blocks = out.rearrange("(b p) r -> p b r", p=P)
-        width = U // TAIL
-        for c in range(TAIL):
-            cols = slice(c * width, (c + 1) * width)
+                if CLS[c][t] == "F":
+                    nc.vector.tensor_tensor(cws[t][:, cols], cresses[t][:].indirect(lags), lw_sb[t][:, cols], ALU.mult)
+                else:
+                    nc.scalar.activation(cls[t][:, cols], cresses[t][:].indirect(lags), ACT.Copy)
+                    (nc.gpsimd if CLS[c][t] == "G" else nc.vector).tensor_tensor(cws[t][:, cols], cls[t][:, cols], lw_sb[t][:, cols], ALU.mult)
+                nc.vector.scalar_tensor_tensor(
+                    hid[:, t], mls[t][:, cols], mat_factor[:, t : t + 1], cws[t][:, cols], ALU.mult, ALU.add
+                )
             grouped = keep.tile([P, width, PACK], BF16, name="hid_grouped%d" % c, align_bytes=64)
-            copy_on(HIL[c], grouped[:], hid[:, :, cols].rearrange("p t r -> p r t"))
+            copy_on(HIL[c], grouped[:], hid[:].rearrange("p t r -> p r t"))
             codes = keep.tile([P, width], U32, name="hid_codes%d" % c, align_bytes=64)
             scales = keep.tile([P, width], U8, name="hid_bytes%d" % c, align_bytes=64)
             nc.vector.quantize_mx(
                 out=codes[:].bitcast(FP8X4), scales=scales[:], in_=grouped[:].rearrange("p r t -> p (r t)")
             )
-            acc = bank(2 + c)
+            acc = bank(c)
             for b in range(N // P):
                 nc.tensor.matmul_mx(
                     out=acc[:, b * width : (b + 1) * width],
@@ -286,3 +271,17 @@ def tile_picked_yvario_gap_p_kernel(
             result = keep.tile([P, N // P, width], F32, name="result%d" % c)
             copy_on(RES[c], result[:].rearrange("p b r -> p (b r)"), acc[:, : N // P * width])
             nc.sync.dma_start(out_blocks[:, :, cols], result[:])
+
+        def second_weights(t):
+            copy_on("S", w2_grouped[:], w2_sb.rearrange("p j n -> p n j"))
+            nc.vector.quantize_mx(
+                out=w2_codes[:].bitcast(FP8X4), scales=w2_bytes[:], in_=w2_grouped[:].rearrange("p n j -> p (n j)")
+            )
+
+        nc.vector.tensor_scalar(mat_factor[:], unit_sb[:], -0.4 / D, None, ALU.mult)
+        stages = {"p": product, "f": front, "r": robust, "m": matheron, "H": hidden, "w": second_weights, "R": lambda t: back(t, 1), "D": lambda t: back(t, 0), "s": square, "i": inverse, "c": cressie}
+        if "p0" not in ORDER:
+            for t in range(PACK):
+                product(t)
+        for item in ORDER:
+            stages[item[0]]([int(x) for x in item[1:]] if item[0] == "i" else int(item[1:] or 0))

@@ -21,12 +21,10 @@ P = 128
 PACK = 4
 BANK = 512
 LIST = 16
-ORDER = "p0 p1 p2 p3 w f0 f1 f2 R0 f3 R1 s0 D0 s1 D1 R2 R3 r0 r1 i01 c0 c1 r2 i2 c2 r3 i3 c3 s2 D2 s3 D3 m0 m1 m2 m3 H0 H1".split()
-ML, CL, SQ, STEP, AC, IL, NN, HIL, RES = "", "", "", "2222", "SVSSSSSS", "VSVS", "SSSS", "SV", "SS"
-SUB = "PPPP"
-CUTS, MLS, CLS = [0,256,512], ["VVVS","VVVS"], ["SSSS","SSFF"]
-SQS = ["VV","VV","VV","VS"]
-TAIL = 2
+ORDER = "p0 p1 p2 p3 w f0 f1 f2 R0 f3 s0 R1 s1 D0 s2 R2 D1 s3 R3 D2 D3 r0 r1 i01 c0 c1 r2 i2 c2 r3 i3 c3 m0 m1 m2 m3 H0 H1".split()
+AC, IL, NN, HIL, RES, MC = "SVSSSSSS", "SVSV", "SSSS", "SV", "SS", "VVVV"
+SQS, CUTS, MLS, CLS = ["SS","VV","GG","GS"], [0,256,512], ["VVVS","VVVS"], ["FFSS","FFSS"]
+STEP = 2
 
 
 def tile_picked_yvario_gap_p_kernel(
@@ -35,7 +33,6 @@ def tile_picked_yvario_gap_p_kernel(
     nc = tc.nc
     with ExitStack() as ctx:
         keep = ctx.enter_context(tc.tile_pool(name="keep", bufs=1))
-        work = ctx.enter_context(tc.tile_pool(name="work", bufs=4))
         psum = ctx.enter_context(tc.psum_pool(name="psum", bufs=1))
 
         def copy_on(engine, dst, src):
@@ -49,21 +46,23 @@ def tile_picked_yvario_gap_p_kernel(
         def bank(n):
             return psum.tile([P, BANK], F32, name="bank%d" % n)
 
+        tiles = range(PACK)
+        halves = range(S // BANK)
         offs_sb = keep.tile([P, S // LIST], U16, name="offs_sb")
         shf_sb = keep.tile([P, S // LIST], U16, name="shf_sb")
         lag_sb = keep.tile([P, U // LIST], U16, name="lag_sb")
         xs_sb = keep.tile([P, T], U8, name="xs_sb", align_bytes=64)
         xw_sb = keep.tile([P, T], I32, name="xw_sb", align_bytes=64)
         w1_sb = keep.tile([P, PACK, H], F32, name="w1_sb")
-        ys = [keep.tile([P, 2 * S], F32, name="y%d" % t) for t in range(PACK)]
-        w2_sb = ys[3][:, S:].rearrange("p (j c) -> p j c", j=PACK)
-        lw_sb = [ys[1 + t // 2][:, S + (t % 2) * U : S + (t % 2 + 1) * U] for t in range(PACK)]
+        ys = [keep.tile([P, S], F32, name="y%d" % t) for t in tiles]
+        w2_sb = keep.tile([P, PACK, N], F32, name="w2_sb")[:]
+        lw_all = keep.tile([P, PACK, U], F32, name="lw_all")
+        lw_sb = [lw_all[:, t] for t in tiles]
         unit_sb = keep.tile([P, PACK], F32, name="unit_sb")
         ident = keep.tile([P, P], F32, name="ident")
 
-        nc.vector.memset(xs_sb[:].bitcast(I32), 0)
+        nc.gpsimd.memset(xs_sb[:].bitcast(I32), 0)
         nc.sync.dma_start(offs_sb[:], offs)
-        nc.sync.dma_start(shf_sb[:], shf)
         for q in range(4):
             nc.sync.dma_start(
                 xs_sb[32 * q : 32 * q + 4, :].bitcast(I32),
@@ -71,16 +70,13 @@ def tile_picked_yvario_gap_p_kernel(
             )
         nc.sync.dma_start(xw_sb[:], x_words[0].rearrange("p c r -> p (c r)").bitcast(I32))
         nc.sync.dma_start(w1_sb[:], w1.rearrange("(p j) c -> p j c", j=PACK))
-        lw_rows = lw.rearrange("(p t) r -> p (t r)", t=PACK)
-        for u in range(2):
-            nc.sync.dma_start(ys[1 + u][:, S:], lw_rows[:, u * S : (u + 1) * S])
+        nc.sync.dma_start(shf_sb[:], shf)
+        nc.sync.dma_start(lw_all[:], lw.rearrange("(p t) r -> p t r", t=PACK))
         nc.sync.dma_start(w2_sb, w2.rearrange("(p j) c -> p j c", j=PACK))
         nc.sync.dma_start(lag_sb[:], lag)
         nc.sync.dma_start(unit_sb[:], unit.rearrange("(p t) o -> p (t o)", t=PACK))
-        nc.gpsimd.memset(ys[0][:, S:], 0.0)
         make_identity(nc, ident[:])
 
-        halves = range(S // BANK)
         x_codes = [keep.tile([P, BANK], U32, name="x_codes%d" % h, align_bytes=64) for h in halves]
         x_bytes = [keep.tile([P, BANK], U8, name="x_bytes%d" % h, align_bytes=64) for h in halves]
         per_bank = BANK // LIST
@@ -93,8 +89,8 @@ def tile_picked_yvario_gap_p_kernel(
 
         w1_dealt = w1_sb[:].rearrange("p j (m t) -> p t m j", t=PACK)
         w1_codes, w1_bytes = [], []
-        for t in range(PACK):
-            grouped = keep.tile([P, P, PACK], BF16, name="w1_grouped%d" % (0 if t == 2 else t), align_bytes=64)
+        for t in tiles:
+            grouped = keep.tile([P, P, PACK], BF16, name="w1_grouped%d" % [0,1,2,3][t], align_bytes=64)
             copy_on(IL[t], grouped[:], w1_dealt[:, t])
             codes = keep.tile([P, P], U32, name="w1_codes%d" % t, align_bytes=64)
             scales = keep.tile([P, P], U8, name="w1_bytes%d" % t, align_bytes=64)
@@ -105,7 +101,6 @@ def tile_picked_yvario_gap_p_kernel(
             w1_bytes.append(scales)
 
         def product(t):
-            y = ys[t]
             for h in halves:
                 acc = bank(2 * t + h)
                 nc.tensor.matmul_mx(
@@ -117,115 +112,91 @@ def tile_picked_yvario_gap_p_kernel(
                     start=True,
                     stop=True,
                 )
-                copy_on(AC[2 * t + h], y[:, h * BANK : (h + 1) * BANK], acc[:])
+                copy_on(AC[2 * t + h], ys[t][:, h * BANK : (h + 1) * BANK], acc[:])
 
         w2_grouped = keep.tile([P, N, PACK], BF16, name="w2_grouped", align_bytes=64)
         w2_codes = keep.tile([P, N], U32, name="w2_codes", align_bytes=64)
         w2_bytes = keep.tile([P, N], U8, name="w2_bytes", align_bytes=64)
         mat_factor = keep.tile([P, PACK], F32, name="mat_factor")
+        wide = lambda name, cols: [keep.tile([P, cols], F32, name="%s%d" % (name, t)) for t in tiles]
+        partners, mags, roots, sqs = wide("partner", S), wide("mag", S), wide("root", S), wide("sq", S)
+        diffs = wide("diff", S)
+        all_sums, cresses, mls, cws, cls = wide("sums", 2 * V), wide("cress", 2 * V), wide("ml", U), wide("cw", U), wide("cl", U)
+        qs = wide("q", V)
+        dens = keep.tile([P, PACK * V], F32, name="dens")
+        inv01 = mags[PACK - 1][:, BANK:]
+        out_blocks = out.rearrange("(b p) r -> p b r", p=P)
         lag_cut = U // 2
         lag_cols = lag_cut // LIST
-        all_sums, qs, cresses, banks = {}, {}, {}, {}
-        mags = [keep.tile([P, S], F32, name="mag%d" % t) for t in range(PACK)]
 
         def front(t):
             y = ys[t]
-            step = int(STEP[t])
-            neg = work.tile([P, S], F32, name="neg", bufs=4)
-            mag = mags[t]
-            diff = work.tile([P, S], F32, name="diff") if SUB[t] == "G" else None
-            root = work.tile([P, S], F32, name="root")
-            sq = work.tile([P, S], F32, name="sq")
             for h in halves:
                 cols = slice(h * BANK, (h + 1) * BANK)
-                nc.vector.tensor_scalar(
-                    neg[:, cols],
-                    y[:].indirect(shf_sb[:, h * per_bank : (h + 1) * per_bank]),
-                    -1.0,
-                    0.0,
-                    ALU.mult,
-                    ALU.add,
-                )
-                if SUB[t] == "G":
-                    nc.gpsimd.tensor_tensor(diff[:, cols], y[:, cols], neg[:, cols], ALU.add)
+                picks = y[:].indirect(shf_sb[:, h * per_bank : (h + 1) * per_bank])
+                nc.vector.tensor_copy(partners[t][:, cols], picks)
+                nc.gpsimd.tensor_tensor(diffs[t][:, cols], y[:, cols], partners[t][:, cols], ALU.subtract)
+                terms = [diffs[t]]
                 dif = bank((2 * t + h) % 6)
-                for b in range(D // step):
-                    for e in range(step):
-                        first = h * BANK + step * P * b
-                        picked = slice(first + e, first + step * P, step)
-                        block = dif[:, (step * b + e) * P : (step * b + e + 1) * P]
-                        if SUB[t] == "G":
-                            nc.tensor.matmul(block, diff[:, picked], ident[:], start=True, stop=True, is_transpose=True)
-                            continue
-                        nc.tensor.matmul(block, y[:, picked], ident[:], start=True, stop=False, is_transpose=True)
-                        nc.tensor.matmul(block, neg[:, picked], ident[:], start=False, stop=True, is_transpose=True)
-                nc.scalar.activation(mag[:, cols], dif[:], ACT.Abs)
-                nc.scalar.activation(root[:, cols], mag[:, cols], ACT.Sqrt, bias=0.05)
+                for b in range(D // STEP):
+                    for e in range(STEP):
+                        first = h * BANK + STEP * P * b
+                        picked = slice(first + e, first + STEP * P, STEP)
+                        block = dif[:, (STEP * b + e) * P : (STEP * b + e + 1) * P]
+                        for k, term in enumerate(terms):
+                            nc.tensor.matmul(
+                                block, term[:, picked], ident[:], start=(k == 0), stop=(k == len(terms) - 1), is_transpose=True
+                            )
+                nc.scalar.activation(mags[t][:, cols], dif[:], ACT.Abs)
+                nc.scalar.activation(roots[t][:, cols], mags[t][:, cols], ACT.Sqrt, bias=0.05)
                 if SQS[t][h] == "S":
-                    nc.scalar.activation(sq[:, cols], dif[:], ACT.Square)
-
-            banks[t] = (root, sq)
+                    nc.scalar.activation(sqs[t][:, cols], dif[:], ACT.Square)
 
         def square(t):
             for h in halves:
                 cols = slice(h * BANK, (h + 1) * BANK)
                 if SQS[t][h] != "S":
-                    (nc.gpsimd if SQS[t][h] == "G" else nc.vector).tensor_tensor(banks[t][1][:, cols], mags[t][:, cols], mags[t][:, cols], ALU.mult)
+                    engine = nc.gpsimd if SQS[t][h] == "G" else nc.vector
+                    engine.tensor_tensor(sqs[t][:, cols], mags[t][:, cols], mags[t][:, cols], ALU.mult)
 
-        for t in range(PACK):
-            all_sums[t] = keep.tile([P, 2 * V], F32, name="sums%d" % t)
+        sum_banks = {}
 
         def back(t, place):
-            src = banks[t][1 - place]
-            pairs = bank(([2,3,4,5], [6,7,6,7])[place][t])
-            for g in range(S // P // 2):
-                for e in range(2):
+            src = (sqs, roots)[place][t]
+            sums = bank(([2,3,4,5], [6,7,6,7])[place][t])[:]
+            for g in range(S // P // STEP):
+                for e in range(STEP):
                     nc.tensor.matmul(
-                        pairs[:, g * P : (g + 1) * P],
-                        src[:, (2 * g + e) * P : (2 * g + e + 1) * P],
+                        sums[:, g * P : (g + 1) * P],
+                        src[:, (STEP * g + e) * P : (STEP * g + e + 1) * P],
                         ident[:],
                         start=(e == 0),
-                        stop=(e == 1),
+                        stop=(e == STEP - 1),
                         is_transpose=True,
                     )
             nc.vector.tensor_reduce(
-                all_sums[t][:, place * V : (place + 1) * V], pairs[:].rearrange("p (v d) -> p v d", d=2), AX.X, ALU.add
+                all_sums[t][:, place * V : (place + 1) * V], sums.rearrange("p (v d) -> p v d", d=2), AX.X, ALU.add
             )
 
-        dens = keep.tile([P, PACK * V], F32, name="dens")
-        inv01 = mags[PACK - 1][:, BANK:]
-        early = (PACK - 1) * V
-
         def robust(t):
-            hold = [9,9,9,9][t]
-            q = mags[hold][:, BANK : BANK + V] if hold < PACK else keep.tile([P, V], F32, name="q%d" % t)[:]
+            q = qs[t][:]
             nc.scalar.activation(q, all_sums[t][:, V:], ACT.Square, scale=1.0 / D)
-            cress = keep.tile([P, 2 * V], F32, name="cress%d" % t)
             nc.scalar.activation(dens[:, t * V : (t + 1) * V], q, ACT.Square, scale=0.5, bias=0.6)
             if NN[t] == "S":
-                nc.scalar.activation(cress[:, V:], q, ACT.Square)
-            elif NN[t] == "G":
-                nc.gpsimd.tensor_tensor(cress[:, V:], q, q, ALU.mult)
+                nc.scalar.activation(cresses[t][:, V:], q, ACT.Square)
             else:
-                nc.vector.tensor_tensor(cress[:, V:], q, q, ALU.mult)
-            cresses[t] = cress
+                (nc.gpsimd if NN[t] == "G" else nc.vector).tensor_tensor(cresses[t][:, V:], q, q, ALU.mult)
 
-        def inverse(tiles):
-            cols = slice(tiles[0] * V, (tiles[-1] + 1) * V)
-            place = inv01 if tiles[0] == 0 else dens[:, (tiles[0] - 2) * V : (tiles[-1] - 1) * V]
+        def inverse(which):
+            cols = slice(which[0] * V, (which[-1] + 1) * V)
+            place = inv01 if which[0] == 0 else dens[:, (which[0] - 2) * V : (which[-1] - 1) * V]
             nc.scalar.activation(place, dens[:, cols], ACT.Abs_reciprocal_sqrt)
 
         def cressie(t):
-            cress = cresses[t]
             inv = inv01[:, t * V : (t + 1) * V] if t < 2 else dens[:, (t - 2) * V : (t - 1) * V]
             nc.vector.scalar_tensor_tensor(
-                cress[:, :V], cress[:, V:], unit_sb[:, t : t + 1], inv, ALU.mult, ALU.mult
+                cresses[t][:, :V], cresses[t][:, V:], unit_sb[:, t : t + 1], inv, ALU.mult, ALU.mult
             )
-
-        mls = [keep.tile([P, U], F32, name="ml%d" % t) for t in range(PACK)]
-        cws = [keep.tile([P, U], F32, name="cw%d" % t) for t in range(PACK)]
-        cls = [keep.tile([P, U], F32, name="cl%d" % t) for t in range(PACK)]
-        out_blocks = out.rearrange("(b p) r -> p b r", p=P)
 
         def matheron(t):
             for c in range(2):
@@ -241,12 +212,12 @@ def tile_picked_yvario_gap_p_kernel(
             width = CUTS[c + 1] - CUTS[c]
             lags = lag_sb[:, CUTS[c] // LIST : CUTS[c + 1] // LIST]
             hid = keep.tile([P, PACK, width], BF16, name="hid%d" % c)
-            for t in range(PACK):
+            for t in tiles:
                 if CLS[c][t] == "F":
                     nc.vector.tensor_tensor(cws[t][:, cols], cresses[t][:].indirect(lags), lw_sb[t][:, cols], ALU.mult)
                 else:
                     nc.scalar.activation(cls[t][:, cols], cresses[t][:].indirect(lags), ACT.Copy)
-                    (nc.gpsimd if CLS[c][t] == "G" else nc.vector).tensor_tensor(cws[t][:, cols], cls[t][:, cols], lw_sb[t][:, cols], ALU.mult)
+                    nc.vector.tensor_tensor(cws[t][:, cols], cls[t][:, cols], lw_sb[t][:, cols], ALU.mult)
                 nc.vector.scalar_tensor_tensor(
                     hid[:, t], mls[t][:, cols], mat_factor[:, t : t + 1], cws[t][:, cols], ALU.mult, ALU.add
                 )
@@ -273,15 +244,13 @@ def tile_picked_yvario_gap_p_kernel(
             nc.sync.dma_start(out_blocks[:, :, cols], result[:])
 
         def second_weights(t):
-            copy_on("S", w2_grouped[:], w2_sb.rearrange("p j n -> p n j"))
+            copy_on("G", w2_grouped[:], w2_sb.rearrange("p j n -> p n j"))
             nc.vector.quantize_mx(
                 out=w2_codes[:].bitcast(FP8X4), scales=w2_bytes[:], in_=w2_grouped[:].rearrange("p n j -> p (n j)")
             )
 
         nc.vector.tensor_scalar(mat_factor[:], unit_sb[:], -0.4 / D, None, ALU.mult)
-        stages = {"p": product, "f": front, "r": robust, "m": matheron, "H": hidden, "w": second_weights, "R": lambda t: back(t, 1), "D": lambda t: back(t, 0), "s": square, "i": inverse, "c": cressie}
-        if "p0" not in ORDER:
-            for t in range(PACK):
-                product(t)
+        stages = {"p": product, "f": front, "r": robust, "m": matheron, "H": hidden, "w": second_weights,
+                  "R": lambda t: back(t, 1), "D": lambda t: back(t, 0), "s": square, "i": inverse, "c": cressie}
         for item in ORDER:
             stages[item[0]]([int(x) for x in item[1:]] if item[0] == "i" else int(item[1:] or 0))

@@ -21,10 +21,10 @@ P = 128
 PACK = 4
 BANK = 512
 LIST = 16
-ORDER = "p0 p1 p2 p3 w f0 f1 f2 R0 f3 s0 R1 s1 D0 s2 R2 D1 s3 R3 D2 D3 r0 r1 i01 c0 c1 r2 i2 c2 r3 i3 c3 m0 m1 m2 m3 H0 H1".split()
-AC, IL, NN, HIL, RES, MC = "SVSSSSSS", "SVSV", "SSSS", "SV", "SS", "VVVV"
-SQS, CUTS, MLS, CLS = ["SS","VV","GG","GS"], [0,256,512], ["VVVS","VVVS"], ["FFSS","FFSS"]
-STEP = 2
+ORDER = "p0 p1 p2 p3 w f0 f1 R0 f2 f3 s0 R1 s1 R2 R3 D0 D1 s2 D2 s3 D3 r0 r1 r2 i012 c0 c1 c2 r3 i3 c3 m0 m1 m2 m3 H0 H1".split()
+AC, IL, NN, HIL, RES, MC = "SVSSSSSS", "SVSS", "VVSS", "SV", "SS", "VVVV"
+SQS, CUTS, MLS, CLS = ["SS","VV","SS","SS"], [0,256,512], ["VVSS","VVSS"], ["FFSS","FFSS"]
+MODE = "2D2D"
 
 
 def tile_picked_yvario_gap_p_kernel(
@@ -53,26 +53,25 @@ def tile_picked_yvario_gap_p_kernel(
         lag_sb = keep.tile([P, U // LIST], U16, name="lag_sb")
         xs_sb = keep.tile([P, T], U8, name="xs_sb", align_bytes=64)
         xw_sb = keep.tile([P, T], I32, name="xw_sb", align_bytes=64)
-        w1_sb = keep.tile([P, PACK, H], F32, name="w1_sb")
-        ys = [keep.tile([P, S], F32, name="y%d" % t) for t in tiles]
-        w2_sb = keep.tile([P, PACK, N], F32, name="w2_sb")[:]
-        lw_all = keep.tile([P, PACK, U], F32, name="lw_all")
-        lw_sb = [lw_all[:, t] for t in tiles]
+        w1_sb = keep.tile([P, PACK, H], F32, name="w_stage")
+        ys = [keep.tile([P, S if t % 2 else 2 * S], F32, name="y%d" % t) for t in tiles]
+        lw_sb = [ys[t // 2 * 2][:, S + (t % 2) * U : S + (t % 2 + 1) * U] for t in tiles]
         unit_sb = keep.tile([P, PACK], F32, name="unit_sb")
         ident = keep.tile([P, P], F32, name="ident")
 
-        nc.gpsimd.memset(xs_sb[:].bitcast(I32), 0)
+        nc.vector.memset(xs_sb[:].bitcast(I32), 0)
         nc.sync.dma_start(offs_sb[:], offs)
+        nc.sync.dma_start(xw_sb[:], x_words[0].rearrange("p c r -> p (c r)").bitcast(I32))
         for q in range(4):
             nc.sync.dma_start(
                 xs_sb[32 * q : 32 * q + 4, :].bitcast(I32),
                 x_scales[0, 4 * q : 4 * q + 4, :].bitcast(I32),
             )
-        nc.sync.dma_start(xw_sb[:], x_words[0].rearrange("p c r -> p (c r)").bitcast(I32))
         nc.sync.dma_start(w1_sb[:], w1.rearrange("(p j) c -> p j c", j=PACK))
         nc.sync.dma_start(shf_sb[:], shf)
-        nc.sync.dma_start(lw_all[:], lw.rearrange("(p t) r -> p t r", t=PACK))
-        nc.sync.dma_start(w2_sb, w2.rearrange("(p j) c -> p j c", j=PACK))
+        lw_rows = lw.rearrange("(p t) r -> p (t r)", t=PACK)
+        for u in range(2):
+            nc.sync.dma_start(ys[2 * u][:, S:], lw_rows[:, u * S : (u + 1) * S])
         nc.sync.dma_start(lag_sb[:], lag)
         nc.sync.dma_start(unit_sb[:], unit.rearrange("(p t) o -> p (t o)", t=PACK))
         make_identity(nc, ident[:])
@@ -80,17 +79,18 @@ def tile_picked_yvario_gap_p_kernel(
         x_codes = [keep.tile([P, BANK], U32, name="x_codes%d" % h, align_bytes=64) for h in halves]
         x_bytes = [keep.tile([P, BANK], U8, name="x_bytes%d" % h, align_bytes=64) for h in halves]
         per_bank = BANK // LIST
-        for h in halves:
-            nc.vector.tensor_copy(x_bytes[h][:], xs_sb[:].indirect(offs_sb[:, h * per_bank : (h + 1) * per_bank]))
-        for h in halves:
+        def look_up(h):
             nc.vector.tensor_copy(
                 x_codes[h][:], xw_sb[:].bitcast(U32).indirect(offs_sb[:, h * per_bank : (h + 1) * per_bank])
             )
+            nc.vector.tensor_copy(x_bytes[h][:], xs_sb[:].indirect(offs_sb[:, h * per_bank : (h + 1) * per_bank]))
+
+        look_up(0)
 
         w1_dealt = w1_sb[:].rearrange("p j (m t) -> p t m j", t=PACK)
         w1_codes, w1_bytes = [], []
         for t in tiles:
-            grouped = keep.tile([P, P, PACK], BF16, name="w1_grouped%d" % [0,1,2,3][t], align_bytes=64)
+            grouped = keep.tile([P, P, PACK], BF16, name="w1_grouped%d" % [0,0,2,3][t], align_bytes=64)
             copy_on(IL[t], grouped[:], w1_dealt[:, t])
             codes = keep.tile([P, P], U32, name="w1_codes%d" % t, align_bytes=64)
             scales = keep.tile([P, P], U8, name="w1_bytes%d" % t, align_bytes=64)
@@ -99,6 +99,8 @@ def tile_picked_yvario_gap_p_kernel(
             )
             w1_codes.append(codes)
             w1_bytes.append(scales)
+            if t == 0:
+                look_up(1)
 
         def product(t):
             for h in halves:
@@ -120,24 +122,34 @@ def tile_picked_yvario_gap_p_kernel(
         mat_factor = keep.tile([P, PACK], F32, name="mat_factor")
         wide = lambda name, cols: [keep.tile([P, cols], F32, name="%s%d" % (name, t)) for t in tiles]
         partners, mags, roots, sqs = wide("partner", S), wide("mag", S), wide("root", S), wide("sq", S)
-        diffs = wide("diff", S)
         all_sums, cresses, mls, cws, cls = wide("sums", 2 * V), wide("cress", 2 * V), wide("ml", U), wide("cw", U), wide("cl", U)
-        qs = wide("q", V)
         dens = keep.tile([P, PACK * V], F32, name="dens")
-        inv01 = mags[PACK - 1][:, BANK:]
+        inv01 = mags[PACK - 1][:, V:]
         out_blocks = out.rearrange("(b p) r -> p b r", p=P)
         lag_cut = U // 2
         lag_cols = lag_cut // LIST
 
+        diffs = wide("diff", S)
+        rsums = wide("rsum", V)
+
         def front(t):
+            diff = diffs[t]
+            STEP = int(MODE[t]) if MODE[t] != "D" else 0
             y = ys[t]
             for h in halves:
                 cols = slice(h * BANK, (h + 1) * BANK)
                 picks = y[:].indirect(shf_sb[:, h * per_bank : (h + 1) * per_bank])
-                nc.vector.tensor_copy(partners[t][:, cols], picks)
-                nc.gpsimd.tensor_tensor(diffs[t][:, cols], y[:, cols], partners[t][:, cols], ALU.subtract)
-                terms = [diffs[t]]
-                dif = bank((2 * t + h) % 6)
+                if str(t) in "13":
+                    nc.vector.tensor_copy(partners[t][:, cols], picks)
+                    nc.vector.tensor_tensor(diff[:, cols], y[:, cols], partners[t][:, cols], ALU.subtract)
+                    nc.scalar.activation(mags[t][:, cols], diff[:, cols], ACT.Abs)
+                    nc.scalar.activation(roots[t][:, cols], mags[t][:, cols], ACT.Sqrt, bias=0.05)
+                    if SQS[t][h] == "S":
+                        nc.scalar.activation(sqs[t][:, cols], diff[:, cols], ACT.Square)
+                    continue
+                nc.vector.tensor_scalar(partners[t][:, cols], picks, -1.0, 0.0, ALU.mult, ALU.add)
+                terms = [y, partners[t]]
+                dif = bank([0,2,4,2][t] + h)
                 for b in range(D // STEP):
                     for e in range(STEP):
                         first = h * BANK + STEP * P * b
@@ -148,22 +160,34 @@ def tile_picked_yvario_gap_p_kernel(
                                 block, term[:, picked], ident[:], start=(k == 0), stop=(k == len(terms) - 1), is_transpose=True
                             )
                 nc.scalar.activation(mags[t][:, cols], dif[:], ACT.Abs)
-                nc.scalar.activation(roots[t][:, cols], mags[t][:, cols], ACT.Sqrt, bias=0.05)
+                if str(t) not in "":
+                    nc.scalar.activation(roots[t][:, cols], mags[t][:, cols], ACT.Sqrt, bias=0.05)
+                elif h == 1:
+                    nc.scalar.activation(roots[t][:], mags[t][:], ACT.Sqrt, bias=0.05)
                 if SQS[t][h] == "S":
                     nc.scalar.activation(sqs[t][:, cols], dif[:], ACT.Square)
 
         def square(t):
+            if str(t) in "012" and SQS[t] == "VV":
+                nc.vector.tensor_tensor(sqs[t][:], mags[t][:], mags[t][:], ALU.mult)
+                return
             for h in halves:
                 cols = slice(h * BANK, (h + 1) * BANK)
                 if SQS[t][h] != "S":
                     engine = nc.gpsimd if SQS[t][h] == "G" else nc.vector
-                    engine.tensor_tensor(sqs[t][:, cols], mags[t][:, cols], mags[t][:, cols], ALU.mult)
+                    src = diffs[t] if str(t) in "13" else mags[t]
+                    engine.tensor_tensor(sqs[t][:, cols], src[:, cols], src[:, cols], ALU.mult)
 
         sum_banks = {}
 
         def back(t, place):
             src = (sqs, roots)[place][t]
-            sums = bank(([2,3,4,5], [6,7,6,7])[place][t])[:]
+            target = rsums[t][:] if place == 1 else all_sums[t][:, :V]
+            if MODE[t] == "D":
+                nc.vector.tensor_reduce(target, src[:].rearrange("p (v d) -> p v d", d=D), AX.X, ALU.add)
+                return
+            STEP = int(MODE[t])
+            sums = bank(([0,1,1,3], [6,7,7,6])[place][t])[:]
             for g in range(S // P // STEP):
                 for e in range(STEP):
                     nc.tensor.matmul(
@@ -174,13 +198,16 @@ def tile_picked_yvario_gap_p_kernel(
                         stop=(e == STEP - 1),
                         is_transpose=True,
                     )
-            nc.vector.tensor_reduce(
-                all_sums[t][:, place * V : (place + 1) * V], sums.rearrange("p (v d) -> p v d", d=2), AX.X, ALU.add
-            )
+            if STEP == 2:
+                nc.vector.tensor_reduce(target, sums.rearrange("p (v d) -> p v d", d=2), AX.X, ALU.add)
+            elif place == 0:
+                copy_on(MC[t], target, sums[:, :V])
+            else:
+                sum_banks[t] = sums[:, :V]
 
         def robust(t):
-            q = qs[t][:]
-            nc.scalar.activation(q, all_sums[t][:, V:], ACT.Square, scale=1.0 / D)
+            q = all_sums[t][:, V:]
+            nc.scalar.activation(q, sum_banks.get(t, rsums[t][:]), ACT.Square, scale=1.0 / D)
             nc.scalar.activation(dens[:, t * V : (t + 1) * V], q, ACT.Square, scale=0.5, bias=0.6)
             if NN[t] == "S":
                 nc.scalar.activation(cresses[t][:, V:], q, ACT.Square)
@@ -189,16 +216,22 @@ def tile_picked_yvario_gap_p_kernel(
 
         def inverse(which):
             cols = slice(which[0] * V, (which[-1] + 1) * V)
-            place = inv01 if which[0] == 0 else dens[:, (which[0] - 2) * V : (which[-1] - 1) * V]
+            place = inv01 if which[0] == 0 else dens[:, :V]
             nc.scalar.activation(place, dens[:, cols], ACT.Abs_reciprocal_sqrt)
 
         def cressie(t):
-            inv = inv01[:, t * V : (t + 1) * V] if t < 2 else dens[:, (t - 2) * V : (t - 1) * V]
+            inv = inv01[:, t * V : (t + 1) * V] if t < 3 else dens[:, :V]
             nc.vector.scalar_tensor_tensor(
                 cresses[t][:, :V], cresses[t][:, V:], unit_sb[:, t : t + 1], inv, ALU.mult, ALU.mult
             )
 
         def matheron(t):
+            if str(t) in "":
+                if MLS[0][t] == "V":
+                    nc.vector.tensor_copy(mls[t][:], all_sums[t][:].indirect(lag_sb[:]))
+                else:
+                    nc.scalar.activation(mls[t][:], all_sums[t][:].indirect(lag_sb[:]), ACT.Copy)
+                return
             for c in range(2):
                 cols = slice(c * lag_cut, (c + 1) * lag_cut)
                 lags = lag_sb[:, c * lag_cols : (c + 1) * lag_cols]
@@ -228,23 +261,27 @@ def tile_picked_yvario_gap_p_kernel(
             nc.vector.quantize_mx(
                 out=codes[:].bitcast(FP8X4), scales=scales[:], in_=grouped[:].rearrange("p r t -> p (r t)")
             )
-            acc = bank(c)
-            for b in range(N // P):
-                nc.tensor.matmul_mx(
-                    out=acc[:, b * width : (b + 1) * width],
-                    lhsT=w2_codes[:, b * P : (b + 1) * P].bitcast(FP8X4),
-                    lhsT_scale=w2_bytes[:, b * P : (b + 1) * P],
-                    rhs=codes[:].bitcast(FP8X4),
-                    rhs_scale=scales[:],
-                    start=True,
-                    stop=True,
-                )
-            result = keep.tile([P, N // P, width], F32, name="result%d" % c)
-            copy_on(RES[c], result[:].rearrange("p b r -> p (b r)"), acc[:, : N // P * width])
-            nc.sync.dma_start(out_blocks[:, :, cols], result[:])
+            for first in range(0, width, lag_cut):
+                part = min(lag_cut, width - first)
+                acc = bank(2 * c + first // lag_cut)
+                for b in range(N // P):
+                    nc.tensor.matmul_mx(
+                        out=acc[:, b * part : (b + 1) * part],
+                        lhsT=w2_codes[:, b * P : (b + 1) * P].bitcast(FP8X4),
+                        lhsT_scale=w2_bytes[:, b * P : (b + 1) * P],
+                        rhs=codes[:, first : first + part].bitcast(FP8X4),
+                        rhs_scale=scales[:, first : first + part],
+                        start=True,
+                        stop=True,
+                    )
+                result = keep.tile([P, N // P, part], F32, name="result%d_%d" % (c, first))
+                copy_on(RES[c], result[:].rearrange("p b r -> p (b r)"), acc[:, : N // P * part])
+                nc.sync.dma_start(out_blocks[:, :, CUTS[c] + first : CUTS[c] + first + part], result[:])
 
         def second_weights(t):
-            copy_on("G", w2_grouped[:], w2_sb.rearrange("p j n -> p n j"))
+            w2_sb = keep.tile([P, PACK, N], F32, name="w_stage")[:]
+            nc.sync.dma_start(w2_sb, w2.rearrange("(p j) c -> p j c", j=PACK))
+            copy_on("S", w2_grouped[:], w2_sb.rearrange("p j n -> p n j"))
             nc.vector.quantize_mx(
                 out=w2_codes[:].bitcast(FP8X4), scales=w2_bytes[:], in_=w2_grouped[:].rearrange("p n j -> p (n j)")
             )

@@ -21,10 +21,12 @@ P = 128
 PACK = 4
 BANK = 512
 LIST = 16
-ORDER = "p0 p1 p2 p3 w f0 f1 R0 f2 f3 s0 R1 s1 R2 R3 D0 D1 s2 D2 s3 D3 r0 r1 r2 i012 c0 c1 c2 r3 i3 c3 m0 m1 m2 m3 H0 H1".split()
-AC, IL, NN, HIL, RES, MC = "SVSSSSSS", "SVSS", "VVSS", "SV", "SS", "VVVV"
-SQS, CUTS, MLS, CLS = ["SS","VV","SS","SS"], [0,256,512], ["VVSS","VVSS"], ["FFSS","FFSS"]
-MODE = "2D2D"
+LAGS = U // 2
+LAST = PACK - 1
+
+PLAIN_TILE = 1
+VECTOR_TILES = 2
+SCALAR_SQUARES = 5
 
 
 def tile_picked_yvario_gap_p_kernel(
@@ -34,30 +36,52 @@ def tile_picked_yvario_gap_p_kernel(
     with ExitStack() as ctx:
         keep = ctx.enter_context(tc.tile_pool(name="keep", bufs=1))
         psum = ctx.enter_context(tc.psum_pool(name="psum", bufs=1))
-
-        def copy_on(engine, dst, src):
-            if engine == "V":
-                nc.vector.tensor_copy(dst, src)
-            elif engine == "G":
-                nc.gpsimd.tensor_copy(dst, src)
-            else:
-                nc.scalar.copy(dst, src)
+        tiles = range(PACK)
+        halves = range(S // BANK)
+        turned = [t for t in tiles if t != PLAIN_TILE]
 
         def bank(n):
             return psum.tile([P, BANK], F32, name="bank%d" % n)
 
-        tiles = range(PACK)
-        halves = range(S // BANK)
+        def per_tile(name, cols):
+            return [keep.tile([P, cols], F32, name="%s%d" % (name, t)) for t in tiles]
+
+        def entries(list_sb, first, count):
+            return list_sb[:, first // LIST : (first + count) // LIST]
+
+        def quantise(name, grouped, cols):
+            codes = keep.tile([P, cols], U32, name=name + "_codes", align_bytes=64)
+            scales = keep.tile([P, cols], U8, name=name + "_bytes", align_bytes=64)
+            nc.vector.quantize_mx(
+                out=codes[:].bitcast(FP8X4), scales=scales[:], in_=grouped[:].rearrange("p c j -> p (c j)")
+            )
+            return codes, scales
+
+        def multiply(acc, lhs, lhs_cols, rhs):
+            nc.tensor.matmul_mx(
+                out=acc,
+                lhsT=lhs[0][:, lhs_cols].bitcast(FP8X4),
+                lhsT_scale=lhs[1][:, lhs_cols],
+                rhs=rhs[0][:].bitcast(FP8X4),
+                rhs_scale=rhs[1][:],
+                start=True,
+                stop=True,
+            )
+
+        def add_turned(block, terms):
+            for n, term in enumerate(terms):
+                nc.tensor.matmul(block, term, ident[:], start=(n == 0), stop=(n == len(terms) - 1), is_transpose=True)
+
         offs_sb = keep.tile([P, S // LIST], U16, name="offs_sb")
         shf_sb = keep.tile([P, S // LIST], U16, name="shf_sb")
         lag_sb = keep.tile([P, U // LIST], U16, name="lag_sb")
         xs_sb = keep.tile([P, T], U8, name="xs_sb", align_bytes=64)
         xw_sb = keep.tile([P, T], I32, name="xw_sb", align_bytes=64)
         w1_sb = keep.tile([P, PACK, H], F32, name="w_stage")
-        ys = [keep.tile([P, S if t % 2 else 2 * S], F32, name="y%d" % t) for t in tiles]
-        lw_sb = [ys[t // 2 * 2][:, S + (t % 2) * U : S + (t % 2 + 1) * U] for t in tiles]
         unit_sb = keep.tile([P, PACK], F32, name="unit_sb")
         ident = keep.tile([P, P], F32, name="ident")
+        ys = [keep.tile([P, S if t == PLAIN_TILE else 2 * S], F32, name="y%d" % t) for t in tiles]
+        lw_sb = [ys[t // 2 * 2][:, S + (t % 2) * U : S + (t % 2 + 1) * U] for t in tiles]
 
         nc.vector.memset(xs_sb[:].bitcast(I32), 0)
         nc.sync.dma_start(offs_sb[:], offs)
@@ -74,220 +98,164 @@ def tile_picked_yvario_gap_p_kernel(
             nc.sync.dma_start(ys[2 * u][:, S:], lw_rows[:, u * S : (u + 1) * S])
         nc.sync.dma_start(lag_sb[:], lag)
         nc.sync.dma_start(unit_sb[:], unit.rearrange("(p t) o -> p (t o)", t=PACK))
+        nc.gpsimd.memset(ys[LAST][:, S:], 0.0)
         make_identity(nc, ident[:])
 
-        x_codes = [keep.tile([P, BANK], U32, name="x_codes%d" % h, align_bytes=64) for h in halves]
-        x_bytes = [keep.tile([P, BANK], U8, name="x_bytes%d" % h, align_bytes=64) for h in halves]
-        per_bank = BANK // LIST
         def look_up(h):
-            nc.vector.tensor_copy(
-                x_codes[h][:], xw_sb[:].bitcast(U32).indirect(offs_sb[:, h * per_bank : (h + 1) * per_bank])
-            )
-            nc.vector.tensor_copy(x_bytes[h][:], xs_sb[:].indirect(offs_sb[:, h * per_bank : (h + 1) * per_bank]))
-
-        look_up(0)
+            codes = keep.tile([P, BANK], U32, name="x_codes%d" % h, align_bytes=64)
+            scales = keep.tile([P, BANK], U8, name="x_bytes%d" % h, align_bytes=64)
+            picks = entries(offs_sb, h * BANK, BANK)
+            nc.vector.tensor_copy(codes[:], xw_sb[:].bitcast(U32).indirect(picks))
+            nc.vector.tensor_copy(scales[:], xs_sb[:].indirect(picks))
+            return codes, scales
 
         w1_dealt = w1_sb[:].rearrange("p j (m t) -> p t m j", t=PACK)
-        w1_codes, w1_bytes = [], []
-        for t in tiles:
-            grouped = keep.tile([P, P, PACK], BF16, name="w1_grouped%d" % [0,0,2,3][t], align_bytes=64)
-            copy_on(IL[t], grouped[:], w1_dealt[:, t])
-            codes = keep.tile([P, P], U32, name="w1_codes%d" % t, align_bytes=64)
-            scales = keep.tile([P, P], U8, name="w1_bytes%d" % t, align_bytes=64)
-            nc.vector.quantize_mx(
-                out=codes[:].bitcast(FP8X4), scales=scales[:], in_=grouped[:].rearrange("p m j -> p (m j)")
-            )
-            w1_codes.append(codes)
-            w1_bytes.append(scales)
-            if t == 0:
-                look_up(1)
 
-        def product(t):
+        def first_weights(t):
+            grouped = keep.tile([P, P, PACK], BF16, name="w1_grouped%d" % (0 if t == 1 else t), align_bytes=64)
+            (nc.vector.tensor_copy if t == 1 else nc.scalar.copy)(grouped[:], w1_dealt[:, t])
+            return quantise("w1_%d" % t, grouped, P)
+
+        x_mx = [look_up(0)]
+        w1_mx = [first_weights(0)]
+        x_mx.append(look_up(1))
+        w1_mx.extend(first_weights(t) for t in tiles if t > 0)
+
+        mat_factor = keep.tile([P, PACK], F32, name="mat_factor")
+        nc.vector.tensor_scalar(mat_factor[:], unit_sb[:], -0.4 / D, None, ALU.mult)
+
+        for t in tiles:
             for h in halves:
                 acc = bank(2 * t + h)
-                nc.tensor.matmul_mx(
-                    out=acc[:],
-                    lhsT=w1_codes[t][:].bitcast(FP8X4),
-                    lhsT_scale=w1_bytes[t][:],
-                    rhs=x_codes[h][:].bitcast(FP8X4),
-                    rhs_scale=x_bytes[h][:],
-                    start=True,
-                    stop=True,
-                )
-                copy_on(AC[2 * t + h], ys[t][:, h * BANK : (h + 1) * BANK], acc[:])
+                multiply(acc[:], w1_mx[t], slice(0, P), x_mx[h])
+                copy_out = nc.vector.tensor_copy if (t, h) == (0, 1) else nc.scalar.copy
+                copy_out(ys[t][:, h * BANK : (h + 1) * BANK], acc[:])
 
+        w2_sb = keep.tile([P, PACK, N], F32, name="w_stage")
+        nc.sync.dma_start(w2_sb[:], w2.rearrange("(p j) c -> p j c", j=PACK))
         w2_grouped = keep.tile([P, N, PACK], BF16, name="w2_grouped", align_bytes=64)
-        w2_codes = keep.tile([P, N], U32, name="w2_codes", align_bytes=64)
-        w2_bytes = keep.tile([P, N], U8, name="w2_bytes", align_bytes=64)
-        mat_factor = keep.tile([P, PACK], F32, name="mat_factor")
-        wide = lambda name, cols: [keep.tile([P, cols], F32, name="%s%d" % (name, t)) for t in tiles]
-        partners, mags, roots, sqs = wide("partner", S), wide("mag", S), wide("root", S), wide("sq", S)
-        all_sums, cresses, mls, cws, cls = wide("sums", 2 * V), wide("cress", 2 * V), wide("ml", U), wide("cw", U), wide("cl", U)
-        dens = keep.tile([P, PACK * V], F32, name="dens")
-        inv01 = mags[PACK - 1][:, V:]
-        out_blocks = out.rearrange("(b p) r -> p b r", p=P)
-        lag_cut = U // 2
-        lag_cols = lag_cut // LIST
+        nc.scalar.copy(w2_grouped[:], w2_sb[:].rearrange("p j n -> p n j"))
+        w2_mx = quantise("w2", w2_grouped, N)
 
-        diffs = wide("diff", S)
-        rsums = wide("rsum", V)
+        partners, mags, roots, squares = (per_tile(name, S) for name in ("partner", "mag", "root", "square"))
+        plain_dif = keep.tile([P, S], F32, name="plain_dif")
 
-        def front(t):
-            diff = diffs[t]
-            STEP = int(MODE[t]) if MODE[t] != "D" else 0
+        def square_on_scalar(t, h):
+            return t != PLAIN_TILE and (2 * t + h < SCALAR_SQUARES or (t, h) == (LAST, 1))
+
+        def differences(t):
             y = ys[t]
             for h in halves:
                 cols = slice(h * BANK, (h + 1) * BANK)
-                picks = y[:].indirect(shf_sb[:, h * per_bank : (h + 1) * per_bank])
-                if str(t) in "13":
-                    nc.vector.tensor_copy(partners[t][:, cols], picks)
-                    nc.vector.tensor_tensor(diff[:, cols], y[:, cols], partners[t][:, cols], ALU.subtract)
-                    nc.scalar.activation(mags[t][:, cols], diff[:, cols], ACT.Abs)
-                    nc.scalar.activation(roots[t][:, cols], mags[t][:, cols], ACT.Sqrt, bias=0.05)
-                    if SQS[t][h] == "S":
-                        nc.scalar.activation(sqs[t][:, cols], diff[:, cols], ACT.Square)
+                picked = y[:].indirect(entries(shf_sb, h * BANK, BANK))
+                if t == PLAIN_TILE:
+                    nc.vector.tensor_copy(partners[t][:, cols], picked)
+                    nc.vector.tensor_tensor(plain_dif[:, cols], y[:, cols], partners[t][:, cols], ALU.subtract)
+                    if h == 1:
+                        nc.scalar.activation(mags[t][:], plain_dif[:], ACT.Abs)
+                        nc.scalar.activation(roots[t][:], mags[t][:], ACT.Sqrt, bias=0.05)
                     continue
-                nc.vector.tensor_scalar(partners[t][:, cols], picks, -1.0, 0.0, ALU.mult, ALU.add)
-                terms = [y, partners[t]]
-                dif = bank([0,2,4,2][t] + h)
-                for b in range(D // STEP):
-                    for e in range(STEP):
-                        first = h * BANK + STEP * P * b
-                        picked = slice(first + e, first + STEP * P, STEP)
-                        block = dif[:, (STEP * b + e) * P : (STEP * b + e + 1) * P]
-                        for k, term in enumerate(terms):
-                            nc.tensor.matmul(
-                                block, term[:, picked], ident[:], start=(k == 0), stop=(k == len(terms) - 1), is_transpose=True
-                            )
+                nc.vector.tensor_scalar(partners[t][:, cols], picked, -1.0, 0.0, ALU.mult, ALU.add)
+                dif = bank(2 * (PLAIN_TILE if t == LAST else t) + h)
+                for b in range(2):
+                    for e in range(2):
+                        first = h * BANK + 2 * P * b
+                        samples = slice(first + e, first + 2 * P, 2)
+                        add_turned(dif[:, (2 * b + e) * P : (2 * b + e + 1) * P], [y[:, samples], partners[t][:, samples]])
                 nc.scalar.activation(mags[t][:, cols], dif[:], ACT.Abs)
-                if str(t) not in "":
+                if t == LAST:
                     nc.scalar.activation(roots[t][:, cols], mags[t][:, cols], ACT.Sqrt, bias=0.05)
                 elif h == 1:
                     nc.scalar.activation(roots[t][:], mags[t][:], ACT.Sqrt, bias=0.05)
-                if SQS[t][h] == "S":
-                    nc.scalar.activation(sqs[t][:, cols], dif[:], ACT.Square)
+                if square_on_scalar(t, h):
+                    nc.scalar.activation(squares[t][:, cols], dif[:], ACT.Square)
 
-        def square(t):
-            if str(t) in "012" and SQS[t] == "VV":
-                nc.vector.tensor_tensor(sqs[t][:], mags[t][:], mags[t][:], ALU.mult)
+        def lag_sums(target, values, t, bank_number):
+            if t == PLAIN_TILE:
+                nc.vector.tensor_reduce(target, values[:].rearrange("p (v d) -> p v d", d=D), AX.X, ALU.add)
                 return
+            pairs = bank(bank_number)
+            for g in range(BANK // P):
+                add_turned(pairs[:, g * P : (g + 1) * P], [values[:, (2 * g + e) * P : (2 * g + e + 1) * P] for e in range(2)])
+            nc.vector.tensor_reduce(target, pairs[:].rearrange("p (v d) -> p v d", d=2), AX.X, ALU.add)
+
+        root_sums, mat_windows, cress_windows = per_tile("root_sum", V), per_tile("mat", 2 * V), per_tile("cress", 2 * V)
+
+        def sum_roots(t):
+            lag_sums(root_sums[t][:], roots[t], t, 2 * LAST + sum(u < t for u in turned) % 2)
+
+        def sum_squares(t):
             for h in halves:
                 cols = slice(h * BANK, (h + 1) * BANK)
-                if SQS[t][h] != "S":
-                    engine = nc.gpsimd if SQS[t][h] == "G" else nc.vector
-                    src = diffs[t] if str(t) in "13" else mags[t]
-                    engine.tensor_tensor(sqs[t][:, cols], src[:, cols], src[:, cols], ALU.mult)
+                if t != PLAIN_TILE and not square_on_scalar(t, h):
+                    nc.vector.tensor_tensor(squares[t][:, cols], mags[t][:, cols], mags[t][:, cols], ALU.mult)
+            lag_sums(mat_windows[t][:, :V], squares[t], t, sum(u < t for u in turned))
 
-        sum_banks = {}
+        for t in tiles:
+            differences(t)
+            if t == PLAIN_TILE:
+                for u in range(PLAIN_TILE):
+                    sum_roots(u)
+        for t in range(PLAIN_TILE, PACK):
+            sum_roots(t)
+            if t == PLAIN_TILE:
+                nc.vector.tensor_tensor(squares[t][:], mags[t][:], mags[t][:], ALU.mult)
+        for t in tiles:
+            sum_squares(t)
 
-        def back(t, place):
-            src = (sqs, roots)[place][t]
-            target = rsums[t][:] if place == 1 else all_sums[t][:, :V]
-            if MODE[t] == "D":
-                nc.vector.tensor_reduce(target, src[:].rearrange("p (v d) -> p v d", d=D), AX.X, ALU.add)
-                return
-            STEP = int(MODE[t])
-            sums = bank(([0,1,1,3], [6,7,7,6])[place][t])[:]
-            for g in range(S // P // STEP):
-                for e in range(STEP):
-                    nc.tensor.matmul(
-                        sums[:, g * P : (g + 1) * P],
-                        src[:, (STEP * g + e) * P : (STEP * g + e + 1) * P],
-                        ident[:],
-                        start=(e == 0),
-                        stop=(e == STEP - 1),
-                        is_transpose=True,
-                    )
-            if STEP == 2:
-                nc.vector.tensor_reduce(target, sums.rearrange("p (v d) -> p v d", d=2), AX.X, ALU.add)
-            elif place == 0:
-                copy_on(MC[t], target, sums[:, :V])
+        den_squares = keep.tile([P, PACK * V], F32, name="den_squares")
+
+        def powers(t):
+            mean_square = mat_windows[t][:, V:]
+            nc.scalar.activation(mean_square, root_sums[t][:], ACT.Square, scale=1.0 / D)
+            nc.scalar.activation(den_squares[:, t * V : (t + 1) * V], mean_square, ACT.Square, scale=0.5, bias=0.6)
+            if t < VECTOR_TILES:
+                nc.vector.tensor_tensor(cress_windows[t][:, V:], mean_square, mean_square, ALU.mult)
             else:
-                sum_banks[t] = sums[:, :V]
+                nc.scalar.activation(cress_windows[t][:, V:], mean_square, ACT.Square)
 
-        def robust(t):
-            q = all_sums[t][:, V:]
-            nc.scalar.activation(q, sum_banks.get(t, rsums[t][:]), ACT.Square, scale=1.0 / D)
-            nc.scalar.activation(dens[:, t * V : (t + 1) * V], q, ACT.Square, scale=0.5, bias=0.6)
-            if NN[t] == "S":
-                nc.scalar.activation(cresses[t][:, V:], q, ACT.Square)
-            else:
-                (nc.gpsimd if NN[t] == "G" else nc.vector).tensor_tensor(cresses[t][:, V:], q, q, ALU.mult)
-
-        def inverse(which):
-            cols = slice(which[0] * V, (which[-1] + 1) * V)
-            place = inv01 if which[0] == 0 else dens[:, :V]
-            nc.scalar.activation(place, dens[:, cols], ACT.Abs_reciprocal_sqrt)
-
-        def cressie(t):
-            inv = inv01[:, t * V : (t + 1) * V] if t < 3 else dens[:, :V]
-            nc.vector.scalar_tensor_tensor(
-                cresses[t][:, :V], cresses[t][:, V:], unit_sb[:, t : t + 1], inv, ALU.mult, ALU.mult
-            )
-
-        def matheron(t):
-            if str(t) in "":
-                if MLS[0][t] == "V":
-                    nc.vector.tensor_copy(mls[t][:], all_sums[t][:].indirect(lag_sb[:]))
-                else:
-                    nc.scalar.activation(mls[t][:], all_sums[t][:].indirect(lag_sb[:]), ACT.Copy)
-                return
-            for c in range(2):
-                cols = slice(c * lag_cut, (c + 1) * lag_cut)
-                lags = lag_sb[:, c * lag_cols : (c + 1) * lag_cols]
-                if MLS[c][t] == "V":
-                    nc.vector.tensor_copy(mls[t][:, cols], all_sums[t][:].indirect(lags))
-                else:
-                    nc.scalar.activation(mls[t][:, cols], all_sums[t][:].indirect(lags), ACT.Copy)
-
-        def hidden(c):
-            cols = slice(CUTS[c], CUTS[c + 1])
-            width = CUTS[c + 1] - CUTS[c]
-            lags = lag_sb[:, CUTS[c] // LIST : CUTS[c + 1] // LIST]
-            hid = keep.tile([P, PACK, width], BF16, name="hid%d" % c)
-            for t in tiles:
-                if CLS[c][t] == "F":
-                    nc.vector.tensor_tensor(cws[t][:, cols], cresses[t][:].indirect(lags), lw_sb[t][:, cols], ALU.mult)
-                else:
-                    nc.scalar.activation(cls[t][:, cols], cresses[t][:].indirect(lags), ACT.Copy)
-                    nc.vector.tensor_tensor(cws[t][:, cols], cls[t][:, cols], lw_sb[t][:, cols], ALU.mult)
+        def robust(group, inverse):
+            for t in group:
+                powers(t)
+            nc.scalar.activation(inverse, den_squares[:, group[0] * V : (group[-1] + 1) * V], ACT.Abs_reciprocal_sqrt)
+            for n, t in enumerate(group):
+                window = cress_windows[t]
                 nc.vector.scalar_tensor_tensor(
-                    hid[:, t], mls[t][:, cols], mat_factor[:, t : t + 1], cws[t][:, cols], ALU.mult, ALU.add
+                    window[:, :V], window[:, V:], unit_sb[:, t : t + 1], inverse[:, n * V : (n + 1) * V], ALU.mult, ALU.mult
                 )
-            grouped = keep.tile([P, width, PACK], BF16, name="hid_grouped%d" % c, align_bytes=64)
-            copy_on(HIL[c], grouped[:], hid[:].rearrange("p t r -> p r t"))
-            codes = keep.tile([P, width], U32, name="hid_codes%d" % c, align_bytes=64)
-            scales = keep.tile([P, width], U8, name="hid_bytes%d" % c, align_bytes=64)
-            nc.vector.quantize_mx(
-                out=codes[:].bitcast(FP8X4), scales=scales[:], in_=grouped[:].rearrange("p r t -> p (r t)")
-            )
-            for first in range(0, width, lag_cut):
-                part = min(lag_cut, width - first)
-                acc = bank(2 * c + first // lag_cut)
-                for b in range(N // P):
-                    nc.tensor.matmul_mx(
-                        out=acc[:, b * part : (b + 1) * part],
-                        lhsT=w2_codes[:, b * P : (b + 1) * P].bitcast(FP8X4),
-                        lhsT_scale=w2_bytes[:, b * P : (b + 1) * P],
-                        rhs=codes[:, first : first + part].bitcast(FP8X4),
-                        rhs_scale=scales[:, first : first + part],
-                        start=True,
-                        stop=True,
-                    )
-                result = keep.tile([P, N // P, part], F32, name="result%d_%d" % (c, first))
-                copy_on(RES[c], result[:].rearrange("p b r -> p (b r)"), acc[:, : N // P * part])
-                nc.sync.dma_start(out_blocks[:, :, CUTS[c] + first : CUTS[c] + first + part], result[:])
 
-        def second_weights(t):
-            w2_sb = keep.tile([P, PACK, N], F32, name="w_stage")[:]
-            nc.sync.dma_start(w2_sb, w2.rearrange("(p j) c -> p j c", j=PACK))
-            copy_on("S", w2_grouped[:], w2_sb.rearrange("p j n -> p n j"))
-            nc.vector.quantize_mx(
-                out=w2_codes[:].bitcast(FP8X4), scales=w2_bytes[:], in_=w2_grouped[:].rearrange("p n j -> p (n j)")
-            )
+        robust(range(LAST), mags[LAST][:, V:])
+        robust([LAST], den_squares[:, :V])
 
-        nc.vector.tensor_scalar(mat_factor[:], unit_sb[:], -0.4 / D, None, ALU.mult)
-        stages = {"p": product, "f": front, "r": robust, "m": matheron, "H": hidden, "w": second_weights,
-                  "R": lambda t: back(t, 1), "D": lambda t: back(t, 0), "s": square, "i": inverse, "c": cressie}
-        for item in ORDER:
-            stages[item[0]]([int(x) for x in item[1:]] if item[0] == "i" else int(item[1:] or 0))
+        pieces = [(slice(c * LAGS, (c + 1) * LAGS), entries(lag_sb, c * LAGS, LAGS)) for c in range(U // LAGS)]
+        mat_lags, weighted = per_tile("mat_lag", U), per_tile("weighted", U)
+        cress_lags = {t: keep.tile([P, U], F32, name="cress_lag%d" % t) for t in tiles if t >= VECTOR_TILES}
+        for t in tiles:
+            for cols, lags in pieces:
+                if t < VECTOR_TILES:
+                    nc.vector.tensor_copy(mat_lags[t][:, cols], mat_windows[t][:].indirect(lags))
+                else:
+                    nc.scalar.activation(mat_lags[t][:, cols], mat_windows[t][:].indirect(lags), ACT.Copy)
+
+        out_blocks = out.rearrange("(b p) r -> p b r", p=P)
+        for c, (cols, lags) in enumerate(pieces):
+            hid = keep.tile([P, PACK, LAGS], BF16, name="hid%d" % c)
+            for t in tiles:
+                if t < VECTOR_TILES:
+                    cress_lag = cress_windows[t][:].indirect(lags)
+                else:
+                    cress_lag = cress_lags[t][:, cols]
+                    nc.scalar.activation(cress_lag, cress_windows[t][:].indirect(lags), ACT.Copy)
+                nc.vector.tensor_tensor(weighted[t][:, cols], cress_lag, lw_sb[t][:, cols], ALU.mult)
+                nc.vector.scalar_tensor_tensor(
+                    hid[:, t], mat_lags[t][:, cols], mat_factor[:, t : t + 1], weighted[t][:, cols], ALU.mult, ALU.add
+                )
+            grouped = keep.tile([P, LAGS, PACK], BF16, name="hid_grouped%d" % c, align_bytes=64)
+            (nc.scalar.copy if c == 0 else nc.vector.tensor_copy)(grouped[:], hid[:].rearrange("p t r -> p r t"))
+            hid_mx = quantise("hid%d" % c, grouped, LAGS)
+            for b in range(N // P):
+                acc = bank(2 * c + b)
+                multiply(acc[:, :LAGS], w2_mx, slice(b * P, (b + 1) * P), hid_mx)
+                result = keep.tile([P, LAGS], F32, name="result%d_%d" % (c, b))
+                (nc.vector.tensor_copy if (c, b) == (1, 1) else nc.scalar.copy)(result[:], acc[:, :LAGS])
+                nc.sync.dma_start(out_blocks[:, b, cols], result[:])

from contextlib import ExitStack

import concourse.mybir as mybir
from concourse.masks import make_identity

K, T, S, D, N, H, V, U = 512, 2048, 1024, 4, 256, 512, 256, 512
FLOPS = 2 * K * H * S + 2 * H * N * U

F32 = mybir.dt.float32
BF16 = mybir.dt.bfloat16
I32 = mybir.dt.int32
U32 = mybir.dt.uint32
U16 = mybir.dt.uint16
U8 = mybir.dt.uint8
FP8X4 = mybir.dt.float8_e4m3fn_x4
ACT = mybir.ActivationFunctionType
ALU = mybir.AluOpType
AX = mybir.AxisListType

P = 128
PACK = 4
BANK = 512
LIST = 16
LAGS = U // 2
LAST = PACK - 1

PLAIN_TILE = 1
VECTOR_TILES = 2
SCALAR_SQUARES = 5


def tile_picked_yvario_gap_p_kernel(
    tc, x_words, x_scales, w1, lw, unit, w2, offs, shf, lag, out
):
    nc = tc.nc
    with ExitStack() as ctx:
        keep = ctx.enter_context(tc.tile_pool(name="keep", bufs=1))
        psum = ctx.enter_context(tc.psum_pool(name="psum", bufs=1))
        tiles = range(PACK)
        halves = range(S // BANK)
        turned = [t for t in tiles if t != PLAIN_TILE]

        def bank(n):
            return psum.tile([P, BANK], F32, name="bank%d" % n)

        def per_tile(name, cols):
            return [keep.tile([P, cols], F32, name="%s%d" % (name, t)) for t in tiles]

        def entries(list_sb, first, count):
            return list_sb[:, first // LIST : (first + count) // LIST]

        def quantise(name, grouped, cols):
            codes = keep.tile([P, cols], U32, name=name + "_codes", align_bytes=64)
            scales = keep.tile([P, cols], U8, name=name + "_bytes", align_bytes=64)
            nc.vector.quantize_mx(
                out=codes[:].bitcast(FP8X4), scales=scales[:], in_=grouped[:].rearrange("p c j -> p (c j)")
            )
            return codes, scales

        def multiply(acc, lhs, lhs_cols, rhs):
            nc.tensor.matmul_mx(
                out=acc,
                lhsT=lhs[0][:, lhs_cols].bitcast(FP8X4),
                lhsT_scale=lhs[1][:, lhs_cols],
                rhs=rhs[0][:].bitcast(FP8X4),
                rhs_scale=rhs[1][:],
                start=True,
                stop=True,
            )

        def add_turned(block, terms):
            for n, term in enumerate(terms):
                nc.tensor.matmul(block, term, ident[:], start=(n == 0), stop=(n == len(terms) - 1), is_transpose=True)

        offs_sb = keep.tile([P, S // LIST], U16, name="offs_sb")
        shf_sb = keep.tile([P, S // LIST], U16, name="shf_sb")
        lag_sb = keep.tile([P, U // LIST], U16, name="lag_sb")
        xs_sb = keep.tile([P, T], U8, name="xs_sb", align_bytes=64)
        xw_sb = keep.tile([P, T], I32, name="xw_sb", align_bytes=64)
        w1_sb = keep.tile([P, PACK, H], F32, name="w_stage")
        unit_sb = keep.tile([P, PACK], F32, name="unit_sb")
        ident = keep.tile([P, P], F32, name="ident")
        ys = [keep.tile([P, S if t == PLAIN_TILE else 2 * S], F32, name="y%d" % t) for t in tiles]
        lw_sb = [ys[t // 2 * 2][:, S + (t % 2) * U : S + (t % 2 + 1) * U] for t in tiles]

        nc.vector.memset(xs_sb[:].bitcast(I32), 0)
        nc.sync.dma_start(offs_sb[:], offs)
        nc.sync.dma_start(xw_sb[:], x_words[0].rearrange("p c r -> p (c r)").bitcast(I32))
        for q in range(4):
            nc.sync.dma_start(
                xs_sb[32 * q : 32 * q + 4, :].bitcast(I32),
                x_scales[0, 4 * q : 4 * q + 4, :].bitcast(I32),
            )
        nc.sync.dma_start(w1_sb[:], w1.rearrange("(p j) c -> p j c", j=PACK))
        nc.sync.dma_start(shf_sb[:], shf)
        lw_rows = lw.rearrange("(p t) r -> p (t r)", t=PACK)
        for u in range(2):
            nc.sync.dma_start(ys[2 * u][:, S:], lw_rows[:, u * S : (u + 1) * S])
        nc.sync.dma_start(lag_sb[:], lag)
        nc.sync.dma_start(unit_sb[:], unit.rearrange("(p t) o -> p (t o)", t=PACK))
        nc.gpsimd.memset(ys[LAST][:, S:], 0.0)
        make_identity(nc, ident[:])

        def look_up(h):
            codes = keep.tile([P, BANK], U32, name="x_codes%d" % h, align_bytes=64)
            scales = keep.tile([P, BANK], U8, name="x_bytes%d" % h, align_bytes=64)
            picks = entries(offs_sb, h * BANK, BANK)
            nc.vector.tensor_copy(codes[:], xw_sb[:].bitcast(U32).indirect(picks))
            nc.vector.tensor_copy(scales[:], xs_sb[:].indirect(picks))
            return codes, scales

        w1_dealt = w1_sb[:].rearrange("p j (m t) -> p t m j", t=PACK)

        def first_weights(t):
            grouped = keep.tile([P, P, PACK], BF16, name="w1_grouped%d" % (0 if t == 1 else t), align_bytes=64)
            (nc.vector.tensor_copy if t == 1 else nc.scalar.copy)(grouped[:], w1_dealt[:, t])
            return quantise("w1_%d" % t, grouped, P)

        x_mx = [look_up(0)]
        w1_mx = [first_weights(0)]
        x_mx.append(look_up(1))
        w1_mx.extend(first_weights(t) for t in tiles if t > 0)

        mat_factor = keep.tile([P, PACK], F32, name="mat_factor")
        nc.vector.tensor_scalar(mat_factor[:], unit_sb[:], -0.4 / D, None, ALU.mult)

        for t in tiles:
            for h in halves:
                acc = bank(2 * t + h)
                multiply(acc[:], w1_mx[t], slice(0, P), x_mx[h])
                copy_out = nc.vector.tensor_copy if (t, h) == (0, 1) else nc.scalar.copy
                copy_out(ys[t][:, h * BANK : (h + 1) * BANK], acc[:])

        w2_sb = keep.tile([P, PACK, N], F32, name="w_stage")
        nc.sync.dma_start(w2_sb[:], w2.rearrange("(p j) c -> p j c", j=PACK))
        w2_grouped = keep.tile([P, N, PACK], BF16, name="w2_grouped", align_bytes=64)
        nc.scalar.copy(w2_grouped[:], w2_sb[:].rearrange("p j n -> p n j"))
        w2_mx = quantise("w2", w2_grouped, N)

        partners, mags, roots, squares = (per_tile(name, S) for name in ("partner", "mag", "root", "square"))
        plain_dif = keep.tile([P, S], F32, name="plain_dif")

        def square_on_scalar(t, h):
            return t != PLAIN_TILE and (2 * t + h < SCALAR_SQUARES or (t, h) == (LAST, 1))

        def differences(t):
            y = ys[t]
            for h in halves:
                cols = slice(h * BANK, (h + 1) * BANK)
                picked = y[:].indirect(entries(shf_sb, h * BANK, BANK))
                if t == PLAIN_TILE:
                    nc.vector.tensor_copy(partners[t][:, cols], picked)
                    nc.vector.tensor_tensor(plain_dif[:, cols], y[:, cols], partners[t][:, cols], ALU.subtract)
                    if h == 1:
                        nc.scalar.activation(mags[t][:], plain_dif[:], ACT.Abs)
                        nc.scalar.activation(roots[t][:], mags[t][:], ACT.Sqrt, bias=0.05)
                    continue
                nc.vector.tensor_scalar(partners[t][:, cols], picked, -1.0, 0.0, ALU.mult, ALU.add)
                dif = bank(2 * (PLAIN_TILE if t == LAST else t) + h)
                for b in range(2):
                    for e in range(2):
                        first = h * BANK + 2 * P * b
                        samples = slice(first + e, first + 2 * P, 2)
                        add_turned(dif[:, (2 * b + e) * P : (2 * b + e + 1) * P], [y[:, samples], partners[t][:, samples]])
                nc.scalar.activation(mags[t][:, cols], dif[:], ACT.Abs)
                if t == LAST:
                    nc.scalar.activation(roots[t][:, cols], mags[t][:, cols], ACT.Sqrt, bias=0.05)
                elif h == 1:
                    nc.scalar.activation(roots[t][:], mags[t][:], ACT.Sqrt, bias=0.05)
                if square_on_scalar(t, h):
                    nc.scalar.activation(squares[t][:, cols], dif[:], ACT.Square)

        def lag_sums(target, values, t, bank_number):
            if t == PLAIN_TILE:
                nc.vector.tensor_reduce(target, values[:].rearrange("p (v d) -> p v d", d=D), AX.X, ALU.add)
                return
            pairs = bank(bank_number)
            for g in range(BANK // P):
                add_turned(pairs[:, g * P : (g + 1) * P], [values[:, (2 * g + e) * P : (2 * g + e + 1) * P] for e in range(2)])
            nc.vector.tensor_reduce(target, pairs[:].rearrange("p (v d) -> p v d", d=2), AX.X, ALU.add)

        root_sums, mat_windows, cress_windows = per_tile("root_sum", V), per_tile("mat", 2 * V), per_tile("cress", 2 * V)

        def sum_roots(t):
            lag_sums(root_sums[t][:], roots[t], t, 2 * LAST + sum(u < t for u in turned) % 2)

        def sum_squares(t):
            for h in halves:
                cols = slice(h * BANK, (h + 1) * BANK)
                if t != PLAIN_TILE and not square_on_scalar(t, h):
                    nc.vector.tensor_tensor(squares[t][:, cols], mags[t][:, cols], mags[t][:, cols], ALU.mult)
            lag_sums(mat_windows[t][:, :V], squares[t], t, sum(u < t for u in turned))

        for t in tiles:
            differences(t)
            if t == PLAIN_TILE:
                for u in range(PLAIN_TILE):
                    sum_roots(u)
        for t in range(PLAIN_TILE, PACK):
            sum_roots(t)
            if t == PLAIN_TILE:
                nc.vector.tensor_tensor(squares[t][:], mags[t][:], mags[t][:], ALU.mult)
        for t in tiles:
            sum_squares(t)

        den_squares = keep.tile([P, PACK * V], F32, name="den_squares")

        def powers(t):
            mean_square = mat_windows[t][:, V:]
            nc.scalar.activation(mean_square, root_sums[t][:], ACT.Square, scale=1.0 / D)
            nc.scalar.activation(den_squares[:, t * V : (t + 1) * V], mean_square, ACT.Square, scale=0.5, bias=0.6)
            if t < VECTOR_TILES:
                nc.vector.tensor_tensor(cress_windows[t][:, V:], mean_square, mean_square, ALU.mult)
            else:
                nc.scalar.activation(cress_windows[t][:, V:], mean_square, ACT.Square)

        def robust(group, inverse):
            for t in group:
                powers(t)
            nc.scalar.activation(inverse, den_squares[:, group[0] * V : (group[-1] + 1) * V], ACT.Abs_reciprocal_sqrt)
            for n, t in enumerate(group):
                window = cress_windows[t]
                nc.vector.scalar_tensor_tensor(
                    window[:, :V], window[:, V:], unit_sb[:, t : t + 1], inverse[:, n * V : (n + 1) * V], ALU.mult, ALU.mult
                )

        robust(range(LAST), mags[LAST][:, V:])
        robust([LAST], den_squares[:, :V])

        pieces = [(slice(c * LAGS, (c + 1) * LAGS), entries(lag_sb, c * LAGS, LAGS)) for c in range(U // LAGS)]
        mat_lags, weighted = per_tile("mat_lag", U), per_tile("weighted", U)
        cress_lags = {t: keep.tile([P, U], F32, name="cress_lag%d" % t) for t in tiles if t >= VECTOR_TILES}
        for t in tiles:
            for cols, lags in pieces:
                if t < VECTOR_TILES:
                    nc.vector.tensor_copy(mat_lags[t][:, cols], mat_windows[t][:].indirect(lags))
                else:
                    nc.scalar.activation(mat_lags[t][:, cols], mat_windows[t][:].indirect(lags), ACT.Copy)

        out_blocks = out.rearrange("(b p) r -> p b r", p=P)
        for c, (cols, lags) in enumerate(pieces):
            hid = keep.tile([P, PACK, LAGS], BF16, name="hid%d" % c)
            for t in tiles:
                if t < VECTOR_TILES:
                    cress_lag = cress_windows[t][:].indirect(lags)
                else:
                    cress_lag = cress_lags[t][:, cols]
                    nc.scalar.activation(cress_lag, cress_windows[t][:].indirect(lags), ACT.Copy)
                nc.vector.tensor_tensor(weighted[t][:, cols], cress_lag, lw_sb[t][:, cols], ALU.mult)
                nc.vector.scalar_tensor_tensor(
                    hid[:, t], mat_lags[t][:, cols], mat_factor[:, t : t + 1], weighted[t][:, cols], ALU.mult, ALU.add
                )
            grouped = keep.tile([P, LAGS, PACK], BF16, name="hid_grouped%d" % c, align_bytes=64)
            (nc.scalar.copy if c == 0 else nc.vector.tensor_copy)(grouped[:], hid[:].rearrange("p t r -> p r t"))
            hid_mx = quantise("hid%d" % c, grouped, LAGS)
            for b in range(N // P):
                acc = bank(2 * c + b)
                multiply(acc[:, :LAGS], w2_mx, slice(b * P, (b + 1) * P), hid_mx)
                result = keep.tile([P, LAGS], F32, name="result%d_%d" % (c, b))
                (nc.vector.tensor_copy if (c, b) == (1, 1) else nc.scalar.copy)(result[:], acc[:, :LAGS])
                nc.sync.dma_start(out_blocks[:, b, cols], result[:])
